import numpy as np
import ml_dtypes


def mxq(x, axis, fmt="e4m3"):
    dtype, down = {"e4m3": (ml_dtypes.float8_e4m3fn, 7), "e5m2": (ml_dtypes.float8_e5m2, 14)}[fmt]
    v = np.moveaxis(np.asarray(x, np.float32).astype(ml_dtypes.bfloat16).astype(np.float64), axis, -1)
    blocks = v.reshape(v.shape[:-1] + (-1, 32))
    amax = np.abs(blocks).max(-1, keepdims=True)
    byte = np.maximum(np.where(amax > 0, np.frexp(amax)[1] - 1 + 127, 0) - down, 1)
    scale = np.exp2(byte - 127.0)
    codes = (blocks / scale).astype(np.float32).astype(dtype).astype(np.float64)
    return np.moveaxis((codes * scale).reshape(v.shape), -1, axis)


WIDE = False


def mx_kscale(k):
    if not WIDE:
        return np.ones(k)
    levels = np.array([10, -10, 5, -5, 0])
    if k % 512:
        return np.exp2(np.random.permutation(np.resize(levels, k // 32))).repeat(32)
    a = np.empty((k // 512, 16))
    for p in range(k // 512):
        a[p, :8] = np.random.permutation(np.resize(levels, 8))
        for g in range(8):
            far = levels[np.abs(levels - a[p, g]) >= 10]
            a[p, g + 8] = far[np.random.randint(len(far))]
    return np.exp2(a.ravel()).repeat(32)


def f64(x):
    return np.asarray(x).astype(np.float64)


def striped(idx):
    return np.tile(idx.reshape(-1, 16).T, (8, 1)).astype(np.uint16)


def unstriped(offs):
    return offs[:16].T.reshape(-1).astype(np.int64)


E2M1 = np.array([0.0, 0.5, 1.0, 1.5, 2.0, 3.0, 4.0, 6.0, -0.0, -0.5, -1.0, -1.5, -2.0, -3.0, -4.0, -6.0])


def pack_weight(w, fmt):
    k, n = w.shape
    w = f64(np.asarray(w, np.float32).astype(ml_dtypes.bfloat16)).reshape(k // 32, 32, n)
    amax = np.abs(w).max(1)
    if fmt == "e4m3":
        byte = np.frexp(amax)[1] - 1 + 127 - 7
    else:
        mant, ex = np.frexp(amax / 6.0)
        byte = np.where(mant > 0.5, ex, ex - 1) + 127
    byte = np.clip(np.where(amax > 0, byte, 1), 1, 254)
    scaled = (w * np.exp2(127.0 - byte)[:, None, :]).reshape(k, n).astype(np.float32)
    by_word = np.ascontiguousarray(scaled.reshape(k // 512, 128, 4, n).transpose(0, 1, 3, 2))
    if fmt == "e4m3":
        words = by_word.astype(ml_dtypes.float8_e4m3fn).view(np.uint8)
    else:
        c = by_word.astype(ml_dtypes.float4_e2m1fn).view(np.uint8) & 0xF
        words = (c[..., 0::2] | (c[..., 1::2] << 4)).reshape(k // 512, 128, 2 * n)
    return np.ascontiguousarray(words), np.ascontiguousarray(byte.astype(np.uint8).reshape(k // 512, 16, n))


def unpack_weight(words, scales, fmt):
    g, _, n = scales.shape
    words = np.ascontiguousarray(words).reshape(g, 128, n, -1)
    if fmt == "e4m3":
        vals = words.view(ml_dtypes.float8_e4m3fn).astype(np.float64)
    else:
        nib = np.empty((g, 128, n, 4), np.uint8)
        nib[..., 0::2] = words & 0xF
        nib[..., 1::2] = words >> 4
        vals = E2M1[nib]
    vals = vals * np.repeat(np.exp2(scales.astype(np.float64) - 127.0), 8, axis=1)[..., None]
    return vals.transpose(0, 1, 3, 2).reshape(g * 512, n)


def silu(v):
    return v / (1.0 + np.exp(-np.maximum(v, -700.0)))


K, T, E, C, H, N = 1536, 1024, 6, 128, 512, 384


def by_expert(wq, xq):
    return np.concatenate([wq[e].T @ xq[:, e * C:(e + 1) * C] for e in range(E)], axis=1)


def setup_inputs():
    n = np.random.standard_normal
    s = mx_kscale(K)[:, None]
    u = mx_kscale(H)
    w1 = [pack_weight(m, "e2m1") for m in n((E + 1, K, H)) / np.sqrt(K) / s[None] * u[None, None, :]]
    w2 = [pack_weight(m, "e2m1") for m in n((E + 1, H, N)) / np.sqrt(H) / u[None, :, None]]
    x = pack_weight(n((K, T)) * s, "e4m3")
    return {
        "x_words": x[0],
        "x_scales": x[1],
        "w1_words": np.stack([m[0] for m in w1]),
        "w1_scales": np.stack([m[1] for m in w1]),
        "w2_words": np.stack([m[0] for m in w2]),
        "w2_scales": np.stack([m[1] for m in w2]),
        "gate": np.tile(np.random.uniform(0.2, 1.0, E * C), (N, 1)).astype(np.float32),
        "offs": striped(np.random.permutation(T)[:E * C]),
    }


def reference(x_words, x_scales, w1_words, w1_scales, w2_words, w2_scales, gate, offs):
    idx = unstriped(offs)
    w1 = np.stack([unpack_weight(w1_words[e], w1_scales[e], "e2m1") for e in range(E + 1)])
    w2 = np.stack([unpack_weight(w2_words[e], w2_scales[e], "e2m1") for e in range(E + 1)])
    w1q, w2q = w1, w2
    xs = unpack_weight(x_words, x_scales, "e4m3")
    hs = silu(w1q[E].T @ xs)
    ys = w2q[E].T @ mxq(hs, 0, "e4m3")
    xq = unpack_weight(x_words, x_scales, "e4m3")[:, idx]
    h = silu(by_expert(w1q, xq))
    y = by_expert(w2q, mxq(h, 0, "e4m3"))
    out = ys
    out[:, idx] += f64(gate) * y
    return out

@@ -1,0 +1,242 @@
+from contextlib import ExitStack
+
+import concourse.mybir as mybir
+from concourse.masks import make_identity
+
+K, T, E, C, H, N = 1536, 1024, 6, 128, 512, 384
+FLOPS = 2 * (T + E * C) * (K * H + H * N)
+
+F32 = mybir.dt.float32
+BF16 = mybir.dt.bfloat16
+I32 = mybir.dt.int32
+U32 = mybir.dt.uint32
+U16 = mybir.dt.uint16
+U8 = mybir.dt.uint8
+FP8X4 = mybir.dt.float8_e4m3fn_x4
+FP4X4 = mybir.dt.float4_e2m1fn_x4
+SILU = mybir.ActivationFunctionType.Silu
+MULT = mybir.AluOpType.mult
+ADD = mybir.AluOpType.add
+
+P = 128
+PASSES = K // 512
+NT = N // P
+S = E * C
+BANK = 512
+GROUPS = ((0, 1), (1, 2), (2, 4), (4, 6))
+
+
+def tile_moe_shr_mlp_silu_kernel(tc, x_words, x_scales, w1_words, w1_scales, w2_words, w2_scales, gate, offs, out):
+    nc = tc.nc
+    with ExitStack() as ctx:
+        keep = ctx.enter_context(tc.tile_pool(name="keep", bufs=1))
+        pa = ctx.enter_context(tc.psum_pool(name="pa", bufs=3))
+        pt = ctx.enter_context(tc.psum_pool(name="pt", bufs=2))
+        py = ctx.enter_context(tc.psum_pool(name="py", bufs=3))
+
+        offsets = keep.tile([P, S // 16], U16, name="offsets")
+        nc.sync.dma_start(offsets[:], offs)
+        xw = [keep.tile([P, T], I32, name="xw%d" % s, align_bytes=64) for s in range(PASSES)]
+        for s in range(PASSES):
+            nc.sync.dma_start(xw[s][:], x_words[s].rearrange("p t r -> p (t r)").bitcast(I32))
+
+        xs = keep.tile([P, PASSES, T], U8, name="xs", align_bytes=64)
+        w1s = keep.tile([P, (E + 1) * PASSES, H], U8, name="w1s", align_bytes=64)
+        w2s = keep.tile([P, E + 1, N], U8, name="w2s", align_bytes=64)
+        zero = keep.tile([P, 1], F32, name="zero")
+        ident = keep.tile([P, P], F32, name="ident")
+        windows = [keep.tile([P, T], F32, name="win%d" % n) for n in range(NT)]
+        gw = keep.tile([P, PASSES, S], U32, name="gw", align_bytes=64)
+        hw = keep.tile([P, S + T], U32, name="hw", align_bytes=64)
+        hs = keep.tile([P, S + T], U8, name="hs", align_bytes=64)
+        ysb = keep.tile([P, NT, S], F32, name="ysb")
+
+        nc.vector.memset(xs[:].bitcast(I32), 0)
+        nc.vector.memset(w1s[:, 0 * PASSES:2 * PASSES, :].bitcast(I32), 0)
+        nc.vector.memset(w1s[:, 6 * PASSES:7 * PASSES, :].bitcast(I32), 0)
+        nc.vector.memset(w2s[:].bitcast(I32), 0)
+        nc.vector.memset(w1s[:, 2 * PASSES:6 * PASSES, :].bitcast(I32), 0)
+        with tc.tile_pool(name="setup", bufs=1) as setup:
+            staged = setup.tile([P, 1], F32, name="staged")
+            nc.vector.memset(staged[:], 0.0)
+            nc.vector.tensor_copy(zero[:], staged[:])
+        late = ctx.enter_context(tc.tile_pool(name="late", bufs=1))
+        make_identity(nc, ident[:])
+
+        w1w = late.tile([P, (E + 1) * PASSES, 2 * H], U8, name="w1w", align_bytes=64)
+        w2w = late.tile([P, E + 1, 2 * N], U8, name="w2w", align_bytes=64)
+        gates = {}
+
+        def load_scales(queue, plane, rows):
+            for r in range(4):
+                queue.dma_start(plane[r:P:32].bitcast(I32), rows[r:16:4].bitcast(I32))
+
+        def load_w1(e0, e1):
+            nc.sync.dma_start(w1w[:, e0 * PASSES:e1 * PASSES, :].bitcast(I32),
+                              w1_words[e0:e1].rearrange("e s p b -> p (e s) b").bitcast(I32))
+
+        def load_w2(e0, e1):
+            nc.sync.dma_start(w2w[:, e0:e1, :].bitcast(I32), w2_words[e0:e1].rearrange("e s p b -> p (e s) b").bitcast(I32))
+
+        def load_gate(e0, e1, n0=0, n1=NT, tag=""):
+            name = "gate%d_%d" % (e0, n0)
+            pool = keep if tag else late
+            g = pool.tile([P, n1 - n0, (e1 - e0) * C], F32, name=name, tag=tag or name)
+            nc.sync.dma_start(g[:], gate[n0 * P:n1 * P, e0 * C:e1 * C].rearrange("(n p) j -> p n j", p=P))
+            for n in range(n0, n1):
+                gates[e0, n] = g[:, n - n0, :]
+
+        w1_rows = w1_scales.rearrange("e s f i -> f (e s) i")
+
+        def load_xs():
+            load_scales(nc.sync, xs, x_scales.rearrange("s f t -> f s t"))
+
+        def load_w1s(e0, e1):
+            load_scales(nc.sync, w1s[:, e0 * PASSES:e1 * PASSES, :], w1_rows[:, e0 * PASSES:e1 * PASSES, :])
+
+        def load_w2s():
+            load_scales(nc.sync, w2s, w2_scales.rearrange("e s f n -> f (e s) n"))
+
+        load_xs()
+        load_w1s(0, 2)
+        load_w1(0, 1)
+        load_w1(1, 2)
+        load_w1(6, 7)
+        load_w1s(6, 7)
+        load_w2s()
+        load_w2(0, 2)
+        load_gate(0, 1)
+        load_w1s(2, 6)
+        load_w1(2, 4)
+        load_gate(1, 2, 0, 2)
+        load_w2(2, E + 1)
+        load_w1(4, 6)
+
+        for n in range(NT):
+            nc.scalar.activation(windows[n][:], zero[:].to_broadcast([P, T]), SILU)
+
+        def group_offsets(g):
+            e0, e1 = GROUPS[g]
+            return offsets[:, e0 * C // 16:e1 * C // 16]
+
+        for s in range(PASSES):
+            nc.vector.tensor_copy(gw[:, s, :], xw[s][:].bitcast(U32).indirect(offsets[:]))
+
+        gs = {}
+
+        def gather(g, tag=""):
+            e0, e1 = GROUPS[g]
+            gs[g] = keep.tile([P, PASSES, (e1 - e0) * C], U8, name="gs%d" % g, tag=tag or "gs%d" % g, align_bytes=64)
+            for s in range(PASSES):
+                nc.vector.tensor_copy(gs[g][:, s, :], xs[:, s, :].indirect(group_offsets(g)))
+
+        hb = {}
+
+        def layer1(i):
+            a = pa.tile([P, H], F32, name="a")
+            for s in range(PASSES):
+                if i < E:
+                    e = i
+                    g = [j for j in range(len(GROUPS)) if GROUPS[j][0] <= e < GROUPS[j][1]][0]
+                    c0 = (e - GROUPS[g][0]) * C
+                    words, scales = gw[:, s, e * C:(e + 1) * C], gs[g][:, s, c0:c0 + C]
+                else:
+                    e = E
+                    t0 = (i - E) * P
+                    words, scales = xw[s][:, t0:t0 + P], xs[:, s, t0:t0 + P]
+                nc.tensor.matmul_mx(
+                    out=a[:], lhsT=words.bitcast(FP8X4), lhsT_scale=scales,
+                    rhs=w1w[:, e * PASSES + s, :].bitcast(FP4X4), rhs_scale=w1s[:, e * PASSES + s, :],
+                    start=(s == 0), stop=(s == PASSES - 1))
+            h = keep.tile([P, 2, P, 2], BF16, name="h%d" % i, tag="h%d" % i)
+            nc.scalar.activation(h[:], a[:].rearrange("t (p u e) -> t u p e", u=2, e=2), SILU)
+            hb[i] = h
+
+        def turn(i0, i1):
+            k = i1 - i0
+            tr = pt.tile([P, 2, 2, P], F32, name="tr")
+            for i in range(i0, i1):
+                words = hb[i][:].rearrange("t u p e -> t (u p e)").bitcast(F32)
+                for w in range(2):
+                    nc.tensor.transpose(tr[:, i - i0, w, :], words[:, w * P:(w + 1) * P], ident[:])
+            grouped = keep.tile([P, 4 * P * k], BF16, name="grouped%d" % i0, tag="grouped%d" % i0, align_bytes=64)
+            nc.scalar.copy(grouped[:].bitcast(F32).rearrange("p (h t w) -> p h t w", h=k, w=2),
+                           tr[:, :k].rearrange("p h w t -> p h t w"))
+            cols = slice(i0 * P, i1 * P)
+            nc.vector.quantize_mx(out=hw[:, cols].bitcast(FP8X4), scales=hs[:, cols], in_=grouped[:])
+
+        def layer2(dst, e, n, cols):
+            nc.tensor.matmul_mx(
+                out=dst, lhsT=w2w[:, e, n * 2 * P:(n + 1) * 2 * P].bitcast(FP4X4),
+                lhsT_scale=w2s[:, e, n * P:(n + 1) * P],
+                rhs=hw[:, cols].bitcast(FP8X4), rhs_scale=hs[:, cols], start=True, stop=True)
+
+        def routed2(e):
+            y = py.tile([P, BANK], F32, name="y")
+            for n in range(NT):
+                layer2(y[:, n * P:(n + 1) * P], e, n, slice(e * C, (e + 1) * C))
+            nc.scalar.copy(ysb[:, :, e * C:(e + 1) * C], y[:, :N].rearrange("p (n j) -> p n j", n=NT))
+
+        def scatter(e0, e1, n):
+            cols = slice(e0 * C, e1 * C)
+            nc.vector.tensor_tensor(windows[n][:].indirect(offsets[:, e0 * C // 16:e1 * C // 16]),
+                                    ysb[:, n, cols], gates[e0, n], MULT)
+
+        def scatters(e0, e1):
+            for n in range(NT):
+                scatter(e0, e1, n)
+
+        def finish(n):
+            for t0 in range(0, T, BANK):
+                y = py.tile([P, BANK], F32, name="y")
+                layer2(y[:], E, n, slice(S + t0, S + t0 + BANK))
+                res = keep.tile([P, BANK], F32, name="res%d_%d" % (n, t0))
+                nc.vector.tensor_tensor(res[:], y[:], windows[n][:, t0:t0 + BANK], ADD)
+                nc.sync.dma_start(out[n * P:(n + 1) * P, t0:t0 + BANK], res[:])
+
+        gather(0)
+        gather(1)
+        gather(2)
+        layer1(0)
+        layer1(1)
+        turn(0, 1)
+        gather(3, "grouped0")
+        layer1(6)
+        turn(1, 2)
+        routed2(0)
+        layer1(7)
+        routed2(1)
+        layer1(8)
+        turn(6, 8)
+        layer1(2)
+        layer1(3)
+        layer1(9)
+        turn(2, 4)
+        load_gate(1, 2, 2, 3, "h3")
+        load_gate(2, 4, 0, 2, "h2")
+        scatters(0, 1)
+        turn(8, 10)
+        routed2(2)
+        routed2(3)
+        layer1(4)
+        layer1(5)
+        layer1(10)
+        turn(4, 6)
+        load_gate(2, 4, 2, 3, "h5")
+        load_gate(4, 6, 0, 2, "h4")
+        scatters(1, 2)
+        layer1(11)
+        routed2(4)
+        routed2(5)
+        layer1(12)
+        turn(10, 12)
+        layer1(13)
+        turn(12, 14)
+        load_gate(4, 6, 2, 3, "h13")
+        scatters(2, 4)
+        scatter(4, 6, 0)
+        scatter(4, 6, 1)
+        finish(0)
+        scatter(4, 6, 2)
+        finish(1)
+        finish(2)

@@ -32,7 +32,9 @@ def tile_moe_shr_mlp_silu_kernel(tc, x_words, x_scales, w1_words, w1_scales, w2_
         keep = ctx.enter_context(tc.tile_pool(name="keep", bufs=1))
         pa = ctx.enter_context(tc.psum_pool(name="pa", bufs=3))
         pt = ctx.enter_context(tc.psum_pool(name="pt", bufs=2))
-        py = ctx.enter_context(tc.psum_pool(name="py", bufs=3))
+        py = ctx.enter_context(tc.psum_pool(name="py", bufs=2))
+
+        pr = ctx.enter_context(tc.psum_pool(name="pr", bufs=1))
 
         offsets = keep.tile([P, S // 16], U16, name="offsets")
         nc.sync.dma_start(offsets[:], offs)
@@ -43,7 +45,7 @@ def tile_moe_shr_mlp_silu_kernel(tc, x_words, x_scales, w1_words, w1_scales, w2_
         xs = keep.tile([P, PASSES, T], U8, name="xs", align_bytes=64)
         w1s = keep.tile([P, (E + 1) * PASSES, H], U8, name="w1s", align_bytes=64)
         w2s = keep.tile([P, E + 1, N], U8, name="w2s", align_bytes=64)
-        zero = keep.tile([P, 1], F32, name="zero")
+        zero = keep.tile([P, 8 * NT], F32, name="zero")
         ident = keep.tile([P, P], F32, name="ident")
         windows = [keep.tile([P, T], F32, name="win%d" % n) for n in range(NT)]
         gw = keep.tile([P, PASSES, S], U32, name="gw", align_bytes=64)
@@ -51,40 +53,41 @@ def tile_moe_shr_mlp_silu_kernel(tc, x_words, x_scales, w1_words, w1_scales, w2_
         hs = keep.tile([P, S + T], U8, name="hs", align_bytes=64)
         ysb = keep.tile([P, NT, S], F32, name="ysb")
 
-        nc.vector.memset(xs[:].bitcast(I32), 0)
-        nc.vector.memset(w1s[:, 0 * PASSES:2 * PASSES, :].bitcast(I32), 0)
-        nc.vector.memset(w1s[:, 6 * PASSES:7 * PASSES, :].bitcast(I32), 0)
-        nc.vector.memset(w2s[:].bitcast(I32), 0)
-        nc.vector.memset(w1s[:, 2 * PASSES:6 * PASSES, :].bitcast(I32), 0)
-        with tc.tile_pool(name="setup", bufs=1) as setup:
-            staged = setup.tile([P, 1], F32, name="staged")
-            nc.vector.memset(staged[:], 0.0)
-            nc.vector.tensor_copy(zero[:], staged[:])
-        late = ctx.enter_context(tc.tile_pool(name="late", bufs=1))
-        make_identity(nc, ident[:])
+        def zero_scales(e0, e1):
+            nc.vector.memset(w1s[:, e0 * PASSES:e1 * PASSES, :].bitcast(I32), 0)
 
-        w1w = late.tile([P, (E + 1) * PASSES, 2 * H], U8, name="w1w", align_bytes=64)
-        w2w = late.tile([P, E + 1, 2 * N], U8, name="w2w", align_bytes=64)
+        def stage(n):
+            with tc.tile_pool(name="setup%d" % n, bufs=1) as setup:
+                staged = setup.tile([P, 1], F32, name="staged")
+                nc.vector.memset(staged[:], 0.0)
+                nc.vector.tensor_copy(zero[:, 8 * n:8 * n + 1], staged[:])
+            return ctx.enter_context(tc.tile_pool(name="late%d" % n, bufs=1))
+
+        w1w, w2w = {}, {}
         gates = {}
 
         def load_scales(queue, plane, rows):
-            for r in range(4):
-                queue.dma_start(plane[r:P:32].bitcast(I32), rows[r:16:4].bitcast(I32))
+            for q in (0, 2, 1, 3):
+                queue.dma_start(plane[32 * q:32 * q + 4].bitcast(I32), rows[4 * q:4 * q + 4].bitcast(I32))
 
-        def load_w1(e0, e1):
-            nc.sync.dma_start(w1w[:, e0 * PASSES:e1 * PASSES, :].bitcast(I32),
-                              w1_words[e0:e1].rearrange("e s p b -> p (e s) b").bitcast(I32))
+        def load_w1(pool, e0, e1):
+            t = pool.tile([P, (e1 - e0) * PASSES, 2 * H], U8, name="w1w%d" % e0, align_bytes=64)
+            nc.sync.dma_start(t[:].bitcast(I32), w1_words[e0:e1].rearrange("e s p b -> p (e s) b").bitcast(I32))
+            for e in range(e0, e1):
+                for s in range(PASSES):
+                    w1w[e, s] = t[:, (e - e0) * PASSES + s, :]
 
-        def load_w2(e0, e1):
-            nc.sync.dma_start(w2w[:, e0:e1, :].bitcast(I32), w2_words[e0:e1].rearrange("e s p b -> p (e s) b").bitcast(I32))
+        def load_w2(pool, e0, e1):
+            t = pool.tile([P, e1 - e0, 2 * N], U8, name="w2w%d" % e0, align_bytes=64)
+            nc.sync.dma_start(t[:].bitcast(I32), w2_words[e0:e1].rearrange("e s p b -> p (e s) b").bitcast(I32))
+            for e in range(e0, e1):
+                w2w[e] = t[:, e - e0, :]
 
-        def load_gate(e0, e1, n0=0, n1=NT, tag=""):
-            name = "gate%d_%d" % (e0, n0)
-            pool = keep if tag else late
-            g = pool.tile([P, n1 - n0, (e1 - e0) * C], F32, name=name, tag=tag or name)
-            nc.sync.dma_start(g[:], gate[n0 * P:n1 * P, e0 * C:e1 * C].rearrange("(n p) j -> p n j", p=P))
-            for n in range(n0, n1):
-                gates[e0, n] = g[:, n - n0, :]
+        def load_gate(pool, e0, e1):
+            g = pool.tile([P, NT, (e1 - e0) * C], F32, name="gate%d" % e0)
+            nc.sync.dma_start(g[:], gate[:, e0 * C:e1 * C].rearrange("(n p) j -> p n j", p=P))
+            for e in range(e0, e1):
+                gates[e] = g[:, :, (e - e0) * C:(e - e0 + 1) * C]
 
         w1_rows = w1_scales.rearrange("e s f i -> f (e s) i")
 
@@ -97,23 +100,35 @@ def tile_moe_shr_mlp_silu_kernel(tc, x_words, x_scales, w1_words, w1_scales, w2_
         def load_w2s():
             load_scales(nc.sync, w2s, w2_scales.rearrange("e s f n -> f (e s) n"))
 
+        nc.vector.memset(xs[:].bitcast(I32), 0)
         load_xs()
-        load_w1s(0, 2)
-        load_w1(0, 1)
-        load_w1(1, 2)
-        load_w1(6, 7)
+        zero_scales(6, 7)
         load_w1s(6, 7)
+        late = stage(0)
+        load_w1(late, 6, 7)
+        zero_scales(0, 3)
+        load_w1s(0, 3)
+        late = stage(1)
+        load_w1(late, 0, 1)
+        load_w1(late, 1, 2)
+        nc.vector.memset(w2s[:].bitcast(I32), 0)
         load_w2s()
-        load_w2(0, 2)
-        load_gate(0, 1)
-        load_w1s(2, 6)
-        load_w1(2, 4)
-        load_gate(1, 2, 0, 2)
-        load_w2(2, E + 1)
-        load_w1(4, 6)
+        load_w2(late, 0, 3)
+        load_gate(late, 0, 1)
+        load_w1(late, 2, 3)
+        zero_scales(3, 6)
+        load_w1s(3, 6)
+        late = stage(2)
+        load_w1(late, 3, 4)
+        load_gate(late, 1, 3)
+        load_w2(late, 3, 7)
+        load_w1(late, 4, 5)
+        load_w1(late, 5, 6)
+        load_gate(late, 3, 6)
+        make_identity(nc, ident[:])
 
         for n in range(NT):
-            nc.scalar.activation(windows[n][:], zero[:].to_broadcast([P, T]), SILU)
+            nc.scalar.activation(windows[n][:], zero[:, 8 * n:8 * n + 1].to_broadcast([P, T]), SILU)
 
         def group_offsets(g):
             e0, e1 = GROUPS[g]
@@ -133,7 +148,7 @@ def tile_moe_shr_mlp_silu_kernel(tc, x_words, x_scales, w1_words, w1_scales, w2_
         hb = {}
 
         def layer1(i):
-            a = pa.tile([P, H], F32, name="a")
+            a = pa.tile([P, H], F32, name="a", tag="a")
             for s in range(PASSES):
                 if i < E:
                     e = i
@@ -146,7 +161,7 @@ def tile_moe_shr_mlp_silu_kernel(tc, x_words, x_scales, w1_words, w1_scales, w2_
                     words, scales = xw[s][:, t0:t0 + P], xs[:, s, t0:t0 + P]
                 nc.tensor.matmul_mx(
                     out=a[:], lhsT=words.bitcast(FP8X4), lhsT_scale=scales,
-                    rhs=w1w[:, e * PASSES + s, :].bitcast(FP4X4), rhs_scale=w1s[:, e * PASSES + s, :],
+                    rhs=w1w[e, s].bitcast(FP4X4), rhs_scale=w1s[:, e * PASSES + s, :],
                     start=(s == 0), stop=(s == PASSES - 1))
             h = keep.tile([P, 2, P, 2], BF16, name="h%d" % i, tag="h%d" % i)
             nc.scalar.activation(h[:], a[:].rearrange("t (p u e) -> t u p e", u=2, e=2), SILU)
@@ -154,7 +169,10 @@ def tile_moe_shr_mlp_silu_kernel(tc, x_words, x_scales, w1_words, w1_scales, w2_
 
         def turn(i0, i1):
             k = i1 - i0
-            tr = pt.tile([P, 2, 2, P], F32, name="tr")
+            if i0 < E:
+                tr = pr.tile([P, 2, 2, P], F32, name="tr", tag="routed")
+            else:
+                tr = pt.tile([P, 2, 2, P], F32, name="tr")
             for i in range(i0, i1):
                 words = hb[i][:].rearrange("t u p e -> t (u p e)").bitcast(F32)
                 for w in range(2):
@@ -167,12 +185,12 @@ def tile_moe_shr_mlp_silu_kernel(tc, x_words, x_scales, w1_words, w1_scales, w2_
 
         def layer2(dst, e, n, cols):
             nc.tensor.matmul_mx(
-                out=dst, lhsT=w2w[:, e, n * 2 * P:(n + 1) * 2 * P].bitcast(FP4X4),
+                out=dst, lhsT=w2w[e][:, n * 2 * P:(n + 1) * 2 * P].bitcast(FP4X4),
                 lhsT_scale=w2s[:, e, n * P:(n + 1) * P],
                 rhs=hw[:, cols].bitcast(FP8X4), rhs_scale=hs[:, cols], start=True, stop=True)
 
         def routed2(e):
-            y = py.tile([P, BANK], F32, name="y")
+            y = pr.tile([P, BANK], F32, name="yr", tag="routed")
             for n in range(NT):
                 layer2(y[:, n * P:(n + 1) * P], e, n, slice(e * C, (e + 1) * C))
             nc.scalar.copy(ysb[:, :, e * C:(e + 1) * C], y[:, :N].rearrange("p (n j) -> p n j", n=NT))
@@ -180,7 +198,7 @@ def tile_moe_shr_mlp_silu_kernel(tc, x_words, x_scales, w1_words, w1_scales, w2_
         def scatter(e0, e1, n):
             cols = slice(e0 * C, e1 * C)
             nc.vector.tensor_tensor(windows[n][:].indirect(offsets[:, e0 * C // 16:e1 * C // 16]),
-                                    ysb[:, n, cols], gates[e0, n], MULT)
+                                    ysb[:, n, cols], gates[e0][:, n, :], MULT)
 
         def scatters(e0, e1):
             for n in range(NT):
@@ -188,7 +206,10 @@ def tile_moe_shr_mlp_silu_kernel(tc, x_words, x_scales, w1_words, w1_scales, w2_
 
         def finish(n):
             for t0 in range(0, T, BANK):
-                y = py.tile([P, BANK], F32, name="y")
+                if n == 0 or (n == NT - 1 and t0 > 0):
+                    y = py.tile([P, BANK], F32, name="y")
+                else:
+                    y = pa.tile([P, BANK], F32, name="ya", tag="a")
                 layer2(y[:], E, n, slice(S + t0, S + t0 + BANK))
                 res = keep.tile([P, BANK], F32, name="res%d_%d" % (n, t0))
                 nc.vector.tensor_tensor(res[:], y[:], windows[n][:, t0:t0 + BANK], ADD)
@@ -197,46 +218,45 @@ def tile_moe_shr_mlp_silu_kernel(tc, x_words, x_scales, w1_words, w1_scales, w2_
         gather(0)
         gather(1)
         gather(2)
+        layer1(6)
+        layer1(7)
         layer1(0)
+        turn(6, 8)
         layer1(1)
         turn(0, 1)
         gather(3, "grouped0")
-        layer1(6)
+        layer1(8)
         turn(1, 2)
         routed2(0)
-        layer1(7)
-        routed2(1)
-        layer1(8)
-        turn(6, 8)
-        layer1(2)
-        layer1(3)
         layer1(9)
-        turn(2, 4)
-        load_gate(1, 2, 2, 3, "h3")
-        load_gate(2, 4, 0, 2, "h2")
-        scatters(0, 1)
+        layer1(2)
         turn(8, 10)
-        routed2(2)
-        routed2(3)
-        layer1(4)
-        layer1(5)
         layer1(10)
-        turn(4, 6)
-        load_gate(2, 4, 2, 3, "h5")
-        load_gate(4, 6, 0, 2, "h4")
-        scatters(1, 2)
+        turn(2, 3)
+        routed2(1)
+        scatters(0, 1)
         layer1(11)
-        routed2(4)
-        routed2(5)
-        layer1(12)
+        layer1(3)
         turn(10, 12)
+        layer1(12)
+        turn(3, 4)
+        routed2(2)
+        scatters(1, 2)
         layer1(13)
+        layer1(4)
         turn(12, 14)
-        load_gate(4, 6, 2, 3, "h13")
-        scatters(2, 4)
-        scatter(4, 6, 0)
-        scatter(4, 6, 1)
+        turn(4, 5)
+        routed2(3)
+        scatters(2, 3)
+        layer1(5)
+        turn(5, 6)
+        routed2(4)
+        scatters(3, 4)
+        routed2(5)
+        scatters(4, 5)
+        scatter(5, 6, 0)
+        scatter(5, 6, 1)
         finish(0)
-        scatter(4, 6, 2)
+        scatter(5, 6, 2)
         finish(1)
         finish(2)

@@ -24,17 +24,17 @@ NT = N // P
 S = E * C
 BANK = 512
 GROUPS = ((0, 1), (1, 2), (2, 4), (4, 6))
+SGROUPS = ((0, 1), (1, 2), (2, 3), (3, 4), (4, 5), (5, 6))
 
 
 def tile_moe_shr_mlp_silu_kernel(tc, x_words, x_scales, w1_words, w1_scales, w2_words, w2_scales, gate, offs, out):
     nc = tc.nc
     with ExitStack() as ctx:
         keep = ctx.enter_context(tc.tile_pool(name="keep", bufs=1))
-        pa = ctx.enter_context(tc.psum_pool(name="pa", bufs=3))
-        pt = ctx.enter_context(tc.psum_pool(name="pt", bufs=2))
-        py = ctx.enter_context(tc.psum_pool(name="py", bufs=2))
+        psum = ctx.enter_context(tc.psum_pool(name="psum", bufs=1))
 
-        pr = ctx.enter_context(tc.psum_pool(name="pr", bufs=1))
+        def bank(b):
+            return psum.tile([P, BANK], F32, name="bank%d" % b, tag="bank%d" % b)
 
         offsets = keep.tile([P, S // 16], U16, name="offsets")
         nc.sync.dma_start(offsets[:], offs)
@@ -45,13 +45,13 @@ def tile_moe_shr_mlp_silu_kernel(tc, x_words, x_scales, w1_words, w1_scales, w2_
         xs = keep.tile([P, PASSES, T], U8, name="xs", align_bytes=64)
         w1s = keep.tile([P, (E + 1) * PASSES, H], U8, name="w1s", align_bytes=64)
         w2s = keep.tile([P, E + 1, N], U8, name="w2s", align_bytes=64)
-        zero = keep.tile([P, 8 * NT], F32, name="zero")
+        zero = keep.tile([P, 1], F32, name="zero")
         ident = keep.tile([P, P], F32, name="ident")
         windows = [keep.tile([P, T], F32, name="win%d" % n) for n in range(NT)]
         gw = keep.tile([P, PASSES, S], U32, name="gw", align_bytes=64)
         hw = keep.tile([P, S + T], U32, name="hw", align_bytes=64)
         hs = keep.tile([P, S + T], U8, name="hs", align_bytes=64)
-        ysb = keep.tile([P, NT, S], F32, name="ysb")
+        ysb = [keep.tile([P, NT, (e1 - e0) * C], F32, name="ysb%d" % e0) for e0, e1 in SGROUPS]
 
         def zero_scales(e0, e1):
             nc.vector.memset(w1s[:, e0 * PASSES:e1 * PASSES, :].bitcast(I32), 0)
@@ -60,7 +60,7 @@ def tile_moe_shr_mlp_silu_kernel(tc, x_words, x_scales, w1_words, w1_scales, w2_
             with tc.tile_pool(name="setup%d" % n, bufs=1) as setup:
                 staged = setup.tile([P, 1], F32, name="staged")
                 nc.vector.memset(staged[:], 0.0)
-                nc.vector.tensor_copy(zero[:, 8 * n:8 * n + 1], staged[:])
+                nc.vector.tensor_copy(zero[:], staged[:])
             return ctx.enter_context(tc.tile_pool(name="late%d" % n, bufs=1))
 
         w1w, w2w = {}, {}
@@ -87,7 +87,7 @@ def tile_moe_shr_mlp_silu_kernel(tc, x_words, x_scales, w1_words, w1_scales, w2_
             g = pool.tile([P, NT, (e1 - e0) * C], F32, name="gate%d" % e0)
             nc.sync.dma_start(g[:], gate[:, e0 * C:e1 * C].rearrange("(n p) j -> p n j", p=P))
             for e in range(e0, e1):
-                gates[e] = g[:, :, (e - e0) * C:(e - e0 + 1) * C]
+                gates[e] = (g, e0)
 
         w1_rows = w1_scales.rearrange("e s f i -> f (e s) i")
 
@@ -100,35 +100,33 @@ def tile_moe_shr_mlp_silu_kernel(tc, x_words, x_scales, w1_words, w1_scales, w2_
         def load_w2s():
             load_scales(nc.sync, w2s, w2_scales.rearrange("e s f n -> f (e s) n"))
 
+        late = keep
         nc.vector.memset(xs[:].bitcast(I32), 0)
         load_xs()
-        zero_scales(6, 7)
-        load_w1s(6, 7)
         late = stage(0)
-        load_w1(late, 6, 7)
-        zero_scales(0, 3)
-        load_w1s(0, 3)
-        late = stage(1)
         load_w1(late, 0, 1)
         load_w1(late, 1, 2)
+        zero_scales(0, 2)
+        load_w1s(0, 2)
+        load_w1(late, 6, 7)
+        load_w1(late, 2, 3)
+        zero_scales(6, 7)
+        load_w1s(6, 7)
+        load_gate(late, 0, 2)
+        load_w2(late, 0, 3)
         nc.vector.memset(w2s[:].bitcast(I32), 0)
         load_w2s()
-        load_w2(late, 0, 3)
-        load_gate(late, 0, 1)
-        load_w1(late, 2, 3)
-        zero_scales(3, 6)
-        load_w1s(3, 6)
-        late = stage(2)
+        zero_scales(2, 6)
+        load_w1s(2, 6)
         load_w1(late, 3, 4)
-        load_gate(late, 1, 3)
-        load_w2(late, 3, 7)
         load_w1(late, 4, 5)
+        load_gate(late, 2, 6)
         load_w1(late, 5, 6)
-        load_gate(late, 3, 6)
+        load_w2(late, 3, 7)
         make_identity(nc, ident[:])
 
         for n in range(NT):
-            nc.scalar.activation(windows[n][:], zero[:, 8 * n:8 * n + 1].to_broadcast([P, T]), SILU)
+            nc.scalar.activation(windows[n][:], zero[:].to_broadcast([P, T]), SILU)
 
         def group_offsets(g):
             e0, e1 = GROUPS[g]
@@ -147,8 +145,8 @@ def tile_moe_shr_mlp_silu_kernel(tc, x_words, x_scales, w1_words, w1_scales, w2_
 
         hb = {}
 
-        def layer1(i):
-            a = pa.tile([P, H], F32, name="a", tag="a")
+        def layer1(i, b):
+            a = bank(b)
             for s in range(PASSES):
                 if i < E:
                     e = i
@@ -167,19 +165,16 @@ def tile_moe_shr_mlp_silu_kernel(tc, x_words, x_scales, w1_words, w1_scales, w2_
             nc.scalar.activation(h[:], a[:].rearrange("t (p u e) -> t u p e", u=2, e=2), SILU)
             hb[i] = h
 
-        def turn(i0, i1):
+        def turn(i0, i1, b):
             k = i1 - i0
-            if i0 < E:
-                tr = pr.tile([P, 2, 2, P], F32, name="tr", tag="routed")
-            else:
-                tr = pt.tile([P, 2, 2, P], F32, name="tr")
+            tr = bank(b)[:].rearrange("p (h w t) -> p h w t", h=2, w=2)
             for i in range(i0, i1):
                 words = hb[i][:].rearrange("t u p e -> t (u p e)").bitcast(F32)
                 for w in range(2):
                     nc.tensor.transpose(tr[:, i - i0, w, :], words[:, w * P:(w + 1) * P], ident[:])
             grouped = keep.tile([P, 4 * P * k], BF16, name="grouped%d" % i0, tag="grouped%d" % i0, align_bytes=64)
             nc.scalar.copy(grouped[:].bitcast(F32).rearrange("p (h t w) -> p h t w", h=k, w=2),
-                           tr[:, :k].rearrange("p h w t -> p h t w"))
+                           tr[:, :k, :, :].rearrange("p h w t -> p h t w"))
             cols = slice(i0 * P, i1 * P)
             nc.vector.quantize_mx(out=hw[:, cols].bitcast(FP8X4), scales=hs[:, cols], in_=grouped[:])
 
@@ -189,74 +184,83 @@ def tile_moe_shr_mlp_silu_kernel(tc, x_words, x_scales, w1_words, w1_scales, w2_
                 lhsT_scale=w2s[:, e, n * P:(n + 1) * P],
                 rhs=hw[:, cols].bitcast(FP8X4), rhs_scale=hs[:, cols], start=True, stop=True)
 
-        def routed2(e):
-            y = pr.tile([P, BANK], F32, name="yr", tag="routed")
+        def routed2(e, b):
+            y = bank(b)
             for n in range(NT):
                 layer2(y[:, n * P:(n + 1) * P], e, n, slice(e * C, (e + 1) * C))
-            nc.scalar.copy(ysb[:, :, e * C:(e + 1) * C], y[:, :N].rearrange("p (n j) -> p n j", n=NT))
+            g = [j for j in range(len(SGROUPS)) if SGROUPS[j][0] <= e < SGROUPS[j][1]][0]
+            c0 = (e - SGROUPS[g][0]) * C
+            nc.scalar.copy(ysb[g][:, :, c0:c0 + C], y[:, :N].rearrange("p (n j) -> p n j", n=NT))
 
-        def scatter(e0, e1, n):
-            cols = slice(e0 * C, e1 * C)
+        def scatter(g, n):
+            e0, e1 = SGROUPS[g]
+            tile, first = gates[e0]
             nc.vector.tensor_tensor(windows[n][:].indirect(offsets[:, e0 * C // 16:e1 * C // 16]),
-                                    ysb[:, n, cols], gates[e0][:, n, :], MULT)
+                                    ysb[g][:, n, :], tile[:, n, (e0 - first) * C:(e1 - first) * C], MULT)
 
-        def scatters(e0, e1):
-            for n in range(NT):
-                scatter(e0, e1, n)
-
-        def finish(n):
-            for t0 in range(0, T, BANK):
-                if n == 0 or (n == NT - 1 and t0 > 0):
-                    y = py.tile([P, BANK], F32, name="y")
-                else:
-                    y = pa.tile([P, BANK], F32, name="ya", tag="a")
-                layer2(y[:], E, n, slice(S + t0, S + t0 + BANK))
-                res = keep.tile([P, BANK], F32, name="res%d_%d" % (n, t0))
-                nc.vector.tensor_tensor(res[:], y[:], windows[n][:, t0:t0 + BANK], ADD)
-                nc.sync.dma_start(out[n * P:(n + 1) * P, t0:t0 + BANK], res[:])
+        def finish(n, t0, t1, b):
+            y = bank(b)
+            layer2(y[:, :t1 - t0], E, n, slice(S + t0, S + t1))
+            res = keep.tile([P, t1 - t0], F32, name="res%d_%d" % (n, t0))
+            nc.vector.tensor_tensor(res[:], y[:, :t1 - t0], windows[n][:, t0:t1], ADD)
+            nc.sync.dma_start(out[n * P:(n + 1) * P, t0:t1], res[:])
 
         gather(0)
+        layer1(9, 5)
+        layer1(0, 3)
+        turn(0, 1, 0)
         gather(1)
+        layer1(1, 4)
+        turn(1, 2, 1)
+        routed2(0, 4)
+        layer1(7, 0)
+        scatter(0, 2)
+        routed2(1, 5)
+        gather(3)
+        layer1(6, 7)
+        turn(6, 8, 1)
         gather(2)
-        layer1(6)
-        layer1(7)
-        layer1(0)
-        turn(6, 8)
-        layer1(1)
-        turn(0, 1)
-        gather(3, "grouped0")
-        layer1(8)
-        turn(1, 2)
-        routed2(0)
-        layer1(9)
-        layer1(2)
-        turn(8, 10)
-        layer1(10)
-        turn(2, 3)
-        routed2(1)
-        scatters(0, 1)
-        layer1(11)
-        layer1(3)
-        turn(10, 12)
-        layer1(12)
-        turn(3, 4)
-        routed2(2)
-        scatters(1, 2)
-        layer1(13)
-        layer1(4)
-        turn(12, 14)
-        turn(4, 5)
-        routed2(3)
-        scatters(2, 3)
-        layer1(5)
-        turn(5, 6)
-        routed2(4)
-        scatters(3, 4)
-        routed2(5)
-        scatters(4, 5)
-        scatter(5, 6, 0)
-        scatter(5, 6, 1)
-        finish(0)
-        scatter(5, 6, 2)
-        finish(1)
-        finish(2)
+        scatter(0, 1)
+        scatter(1, 1)
+        layer1(8, 7)
+        layer1(2, 0)
+        turn(2, 3, 6)
+        routed2(2, 2)
+        layer1(3, 5)
+        scatter(0, 0)
+        layer1(4, 4)
+        layer1(10, 4)
+        turn(3, 4, 5)
+        scatter(1, 0)
+        turn(4, 5, 5)
+        routed2(3, 7)
+        scatter(1, 2)
+        scatter(2, 0)
+        layer1(5, 2)
+        turn(5, 6, 2)
+        scatter(3, 0)
+        layer1(11, 5)
+        scatter(2, 1)
+        routed2(4, 6)
+        layer1(13, 2)
+        layer1(12, 6)
+        routed2(5, 5)
+        scatter(3, 1)
+        scatter(3, 2)
+        turn(10, 12, 1)
+        scatter(4, 0)
+        scatter(5, 0)
+        scatter(4, 1)
+        scatter(5, 1)
+        turn(12, 14, 7)
+        finish(0, 512, 1024, 1)
+        scatter(4, 2)
+        scatter(2, 2)
+        scatter(5, 2)
+        finish(1, 512, 1024, 6)
+        turn(8, 10, 0)
+        finish(1, 0, 512, 2)
+        finish(2, 0, 512, 3)
+        finish(0, 0, 512, 5)
+        finish(2, 512, 768, 7)
+        finish(2, 768, 1024, 4)

@@ -45,7 +45,7 @@ def tile_moe_shr_mlp_silu_kernel(tc, x_words, x_scales, w1_words, w1_scales, w2_
         xs = keep.tile([P, PASSES, T], U8, name="xs", align_bytes=64)
         w1s = keep.tile([P, (E + 1) * PASSES, H], U8, name="w1s", align_bytes=64)
         w2s = keep.tile([P, E + 1, N], U8, name="w2s", align_bytes=64)
-        zero = keep.tile([P, 1], F32, name="zero")
+        zero = keep.tile([P, 8 * NT], F32, name="zero")
         ident = keep.tile([P, P], F32, name="ident")
         windows = [keep.tile([P, T], F32, name="win%d" % n) for n in range(NT)]
         gw = keep.tile([P, PASSES, S], U32, name="gw", align_bytes=64)
@@ -60,15 +60,20 @@ def tile_moe_shr_mlp_silu_kernel(tc, x_words, x_scales, w1_words, w1_scales, w2_
             with tc.tile_pool(name="setup%d" % n, bufs=1) as setup:
                 staged = setup.tile([P, 1], F32, name="staged")
                 nc.vector.memset(staged[:], 0.0)
-                nc.vector.tensor_copy(zero[:], staged[:])
+                nc.vector.tensor_copy(zero[:, 8 * n:8 * n + 1], staged[:])
             return ctx.enter_context(tc.tile_pool(name="late%d" % n, bufs=1))
 
         w1w, w2w = {}, {}
         gates = {}
 
-        def load_scales(queue, plane, rows):
-            for q in (0, 2, 1, 3):
-                queue.dma_start(plane[32 * q:32 * q + 4].bitcast(I32), rows[4 * q:4 * q + 4].bitcast(I32))
+        def load_scales(mode, plane, rows):
+            if mode == 2:
+                for r in range(4):
+                    nc.sync.dma_start(plane[r:P:32].bitcast(I32), rows[r:16:4].bitcast(I32))
+            else:
+                for q in (0, 2, 1, 3):
+                    queue = nc.scalar if mode == 1 and q >= 2 else nc.sync
+                    queue.dma_start(plane[32 * q:32 * q + 4].bitcast(I32), rows[4 * q:4 * q + 4].bitcast(I32))
 
         def load_w1(pool, e0, e1):
             t = pool.tile([P, (e1 - e0) * PASSES, 2 * H], U8, name="w1w%d" % e0, align_bytes=64)
@@ -91,42 +96,45 @@ def tile_moe_shr_mlp_silu_kernel(tc, x_words, x_scales, w1_words, w1_scales, w2_
 
         w1_rows = w1_scales.rearrange("e s f i -> f (e s) i")
 
-        def load_xs():
-            load_scales(nc.sync, xs, x_scales.rearrange("s f t -> f s t"))
+        def load_xs(mode):
+            load_scales(mode, xs, x_scales.rearrange("s f t -> f s t"))
 
-        def load_w1s(e0, e1):
-            load_scales(nc.sync, w1s[:, e0 * PASSES:e1 * PASSES, :], w1_rows[:, e0 * PASSES:e1 * PASSES, :])
+        def load_w1s(e0, e1, mode):
+            load_scales(mode, w1s[:, e0 * PASSES:e1 * PASSES, :], w1_rows[:, e0 * PASSES:e1 * PASSES, :])
 
-        def load_w2s():
-            load_scales(nc.sync, w2s, w2_scales.rearrange("e s f n -> f (e s) n"))
+        def load_w2s(mode):
+            load_scales(mode, w2s, w2_scales.rearrange("e s f n -> f (e s) n"))
 
         late = keep
         nc.vector.memset(xs[:].bitcast(I32), 0)
-        load_xs()
+        load_xs(0)
         late = stage(0)
+        load_w1(late, 6, 7)
+        zero_scales(6, 7)
+        load_w1s(6, 7, 0)
         load_w1(late, 0, 1)
         load_w1(late, 1, 2)
-        zero_scales(0, 2)
-        load_w1s(0, 2)
-        load_w1(late, 6, 7)
+        late = stage(1)
+        zero_scales(0, 3)
+        load_w1s(0, 3, 0)
         load_w1(late, 2, 3)
-        zero_scales(6, 7)
-        load_w1s(6, 7)
-        load_gate(late, 0, 2)
-        load_w2(late, 0, 3)
-        nc.vector.memset(w2s[:].bitcast(I32), 0)
-        load_w2s()
-        zero_scales(2, 6)
-        load_w1s(2, 6)
         load_w1(late, 3, 4)
-        load_w1(late, 4, 5)
-        load_gate(late, 2, 6)
+        load_gate(late, 1, 3)
+        nc.vector.memset(w2s[:].bitcast(I32), 0)
+        load_w2s(0)
+        load_w2(late, 0, 3)
+        zero_scales(3, 6)
+        load_w1s(3, 6, 0)
+        load_gate(late, 0, 1)
+        late = stage(2)
         load_w1(late, 5, 6)
+        load_w1(late, 4, 5)
         load_w2(late, 3, 7)
+        load_gate(late, 3, 6)
         make_identity(nc, ident[:])
 
         for n in range(NT):
-            nc.scalar.activation(windows[n][:], zero[:].to_broadcast([P, T]), SILU)
+            nc.scalar.activation(windows[n][:], zero[:, 8 * n:8 * n + 1].to_broadcast([P, T]), SILU)
 
         def group_offsets(g):
             e0, e1 = GROUPS[g]
@@ -206,61 +214,60 @@ def tile_moe_shr_mlp_silu_kernel(tc, x_words, x_scales, w1_words, w1_scales, w2_
             nc.sync.dma_start(out[n * P:(n + 1) * P, t0:t1], res[:])
 
         gather(0)
-        layer1(9, 5)
-        layer1(0, 3)
-        turn(0, 1, 0)
-        gather(1)
-        layer1(1, 4)
-        turn(1, 2, 1)
-        routed2(0, 4)
-        layer1(7, 0)
-        scatter(0, 2)
-        routed2(1, 5)
-        gather(3)
-        layer1(6, 7)
-        turn(6, 8, 1)
-        gather(2)
-        scatter(0, 1)
-        scatter(1, 1)
         layer1(8, 7)
-        layer1(2, 0)
-        turn(2, 3, 6)
-        routed2(2, 2)
-        layer1(3, 5)
-        scatter(0, 0)
-        layer1(4, 4)
-        layer1(10, 4)
-        turn(3, 4, 5)
+        layer1(6, 3)
+        layer1(7, 4)
+        gather(1)
+        turn(6, 8, 5)
+        layer1(1, 4)
+        layer1(0, 2)
+        layer1(9, 3)
+        turn(1, 2, 5)
+        turn(0, 1, 2)
+        routed2(0, 1)
+        gather(2)
+        layer1(2, 6)
+        routed2(1, 2)
+        turn(2, 3, 4)
+        scatter(1, 1)
+        layer1(3, 6)
+        turn(3, 4, 3)
+        layer1(13, 0)
+        scatter(0, 2)
+        turn(8, 10, 5)
+        layer1(10, 2)
+        gather(3)
         scatter(1, 0)
-        turn(4, 5, 5)
-        routed2(3, 7)
+        routed2(2, 3)
+        scatter(0, 0)
+        scatter(0, 1)
+        layer1(11, 1)
+        layer1(5, 0)
         scatter(1, 2)
+        layer1(4, 6)
         scatter(2, 0)
-        layer1(5, 2)
-        turn(5, 6, 2)
-        scatter(3, 0)
-        layer1(11, 5)
+        turn(5, 6, 1)
+        routed2(3, 7)
         scatter(2, 1)
-        routed2(4, 6)
-        layer1(13, 2)
-        layer1(12, 6)
-        routed2(5, 5)
-        scatter(3, 1)
-        scatter(3, 2)
-        turn(10, 12, 1)
-        scatter(4, 0)
-        scatter(5, 0)
-        scatter(4, 1)
-        scatter(5, 1)
-        turn(12, 14, 7)
-        finish(0, 512, 1024, 1)
-        scatter(4, 2)
         scatter(2, 2)
+        turn(10, 12, 5)
+        turn(4, 5, 2)
+        routed2(5, 5)
+        scatter(3, 0)
+        scatter(3, 2)
+        layer1(12, 7)
+        scatter(3, 1)
+        routed2(4, 1)
         scatter(5, 2)
-        finish(1, 512, 1024, 6)
-        turn(8, 10, 0)
-        finish(1, 0, 512, 2)
-        finish(2, 0, 512, 3)
-        finish(0, 0, 512, 5)
-        finish(2, 512, 768, 7)
-        finish(2, 768, 1024, 4)
+        scatter(5, 0)
+        turn(12, 14, 0)
+        scatter(5, 1)
+        scatter(4, 2)
+        scatter(4, 0)
+        finish(2, 512, 1024, 6)
+        finish(2, 0, 512, 2)
+        scatter(4, 1)
+        finish(0, 0, 512, 7)
+        finish(1, 0, 512, 1)
+        finish(0, 512, 1024, 0)
+        finish(1, 512, 1024, 3)

@@ -23,8 +23,9 @@ PASSES = K // 512
 NT = N // P
 S = E * C
 BANK = 512
-GROUPS = ((0, 1), (1, 2), (2, 4), (4, 6))
-SGROUPS = ((0, 1), (1, 2), (2, 3), (3, 4), (4, 5), (5, 6))
+FIRST = 3
+WARM = 6
+EARLY = 3
 
 
 def tile_moe_shr_mlp_silu_kernel(tc, x_words, x_scales, w1_words, w1_scales, w2_words, w2_scales, gate, offs, out):
@@ -36,25 +37,14 @@ def tile_moe_shr_mlp_silu_kernel(tc, x_words, x_scales, w1_words, w1_scales, w2_
         def bank(b):
             return psum.tile([P, BANK], F32, name="bank%d" % b, tag="bank%d" % b)
 
-        offsets = keep.tile([P, S // 16], U16, name="offsets")
-        nc.sync.dma_start(offsets[:], offs)
-        xw = [keep.tile([P, T], I32, name="xw%d" % s, align_bytes=64) for s in range(PASSES)]
-        for s in range(PASSES):
-            nc.sync.dma_start(xw[s][:], x_words[s].rearrange("p t r -> p (t r)").bitcast(I32))
+        def slots(e0, e1):
+            return offsets[:, e0 * C // 16:e1 * C // 16]
 
-        xs = keep.tile([P, PASSES, T], U8, name="xs", align_bytes=64)
-        w1s = keep.tile([P, (E + 1) * PASSES, H], U8, name="w1s", align_bytes=64)
-        w2s = keep.tile([P, E + 1, N], U8, name="w2s", align_bytes=64)
         zero = keep.tile([P, 8 * NT], F32, name="zero")
-        ident = keep.tile([P, P], F32, name="ident")
         windows = [keep.tile([P, T], F32, name="win%d" % n) for n in range(NT)]
-        gw = keep.tile([P, PASSES, S], U32, name="gw", align_bytes=64)
-        hw = keep.tile([P, S + T], U32, name="hw", align_bytes=64)
-        hs = keep.tile([P, S + T], U8, name="hs", align_bytes=64)
-        ysb = [keep.tile([P, NT, (e1 - e0) * C], F32, name="ysb%d" % e0) for e0, e1 in SGROUPS]
 
-        def zero_scales(e0, e1):
-            nc.vector.memset(w1s[:, e0 * PASSES:e1 * PASSES, :].bitcast(I32), 0)
+        def clear_window(n):
+            nc.scalar.activation(windows[n][:], zero[:, 8 * n:8 * n + 1].to_broadcast([P, T]), SILU)
 
         def stage(n):
             with tc.tile_pool(name="setup%d" % n, bufs=1) as setup:
@@ -63,111 +53,111 @@ def tile_moe_shr_mlp_silu_kernel(tc, x_words, x_scales, w1_words, w1_scales, w2_
                 nc.vector.tensor_copy(zero[:, 8 * n:8 * n + 1], staged[:])
             return ctx.enter_context(tc.tile_pool(name="late%d" % n, bufs=1))
 
-        w1w, w2w = {}, {}
-        gates = {}
+        def load_scales(plane, rows, queue=nc.sync):
+            for q in (0, 2, 1, 3):
+                queue.dma_start(plane[32 * q:32 * q + 4].bitcast(I32), rows[4 * q:4 * q + 4].bitcast(I32))
 
-        def load_scales(mode, plane, rows):
-            if mode == 2:
-                for r in range(4):
-                    nc.sync.dma_start(plane[r:P:32].bitcast(I32), rows[r:16:4].bitcast(I32))
-            else:
-                for q in (0, 2, 1, 3):
-                    queue = nc.scalar if mode == 1 and q >= 2 else nc.sync
-                    queue.dma_start(plane[32 * q:32 * q + 4].bitcast(I32), rows[4 * q:4 * q + 4].bitcast(I32))
+        w1w, w1s, w2w, gates = {}, {}, {}, {}
 
-        def load_w1(pool, e0, e1):
-            t = pool.tile([P, (e1 - e0) * PASSES, 2 * H], U8, name="w1w%d" % e0, align_bytes=64)
-            nc.sync.dma_start(t[:].bitcast(I32), w1_words[e0:e1].rearrange("e s p b -> p (e s) b").bitcast(I32))
+        def load_w1(tile, first, e):
+            rows = tile[:, (e - first) * PASSES:(e - first + 1) * PASSES, :]
+            nc.sync.dma_start(rows.bitcast(I32), w1_words[e].rearrange("s p b -> p s b").bitcast(I32))
+            for s in range(PASSES):
+                w1w[e, s] = tile[:, (e - first) * PASSES + s, :]
+
+        def load_w1s(pool, engine, e0, e1):
+            t = pool.tile([P, (e1 - e0) * PASSES, H], U8, name="w1s%d" % e0, align_bytes=64)
+            engine.memset(t[:].bitcast(I32), 0)
+            load_scales(t, w1_scales[e0:e1].rearrange("e s f i -> f (e s) i"))
             for e in range(e0, e1):
                 for s in range(PASSES):
-                    w1w[e, s] = t[:, (e - e0) * PASSES + s, :]
+                    w1s[e, s] = t[:, (e - e0) * PASSES + s, :]
 
-        def load_w2(pool, e0, e1):
-            t = pool.tile([P, e1 - e0, 2 * N], U8, name="w2w%d" % e0, align_bytes=64)
+        def load_w2(pool, tag, e0, e1):
+            t = pool.tile([P, e1 - e0, 2 * N], U8, name="w2w%d" % e0, tag=tag, align_bytes=64)
             nc.sync.dma_start(t[:].bitcast(I32), w2_words[e0:e1].rearrange("e s p b -> p (e s) b").bitcast(I32))
             for e in range(e0, e1):
                 w2w[e] = t[:, e - e0, :]
 
-        def load_gate(pool, e0, e1):
-            g = pool.tile([P, NT, (e1 - e0) * C], F32, name="gate%d" % e0)
-            nc.sync.dma_start(g[:], gate[:, e0 * C:e1 * C].rearrange("(n p) j -> p n j", p=P))
+        def load_gate(pool, tag, e0, e1):
+            g = pool.tile([P, (e1 - e0) * C], F32, name="gate%d" % e0, tag=tag, align_bytes=64)
+            nc.sync.dma_start(g[:], gate[:P, e0 * C:e1 * C])
             for e in range(e0, e1):
-                gates[e] = (g, e0)
+                gates[e] = g[:, (e - e0) * C:(e - e0 + 1) * C]
 
-        w1_rows = w1_scales.rearrange("e s f i -> f (e s) i")
-
-        def load_xs(mode):
-            load_scales(mode, xs, x_scales.rearrange("s f t -> f s t"))
-
-        def load_w1s(e0, e1, mode):
-            load_scales(mode, w1s[:, e0 * PASSES:e1 * PASSES, :], w1_rows[:, e0 * PASSES:e1 * PASSES, :])
-
-        def load_w2s(mode):
-            load_scales(mode, w2s, w2_scales.rearrange("e s f n -> f (e s) n"))
-
-        late = keep
+        offsets = keep.tile([P, S // 16], U16, name="offsets")
+        nc.sync.dma_start(offsets[:], offs)
+        w1a = keep.tile([P, PASSES, 2 * H], U8, name="w1a", tag="w1a", align_bytes=64)
+        load_w1(w1a, 0, 0)
+        x_rows = x_words.rearrange("s p t r -> p s (t r)").bitcast(I32)
+        xa = keep.tile([P, T], I32, name="xa", align_bytes=64)
+        nc.sync.dma_start(xa[:], x_rows[:, 0, :])
+        xs = keep.tile([P, PASSES, T], U8, name="xs", align_bytes=64)
         nc.vector.memset(xs[:].bitcast(I32), 0)
-        load_xs(0)
+        load_scales(xs, x_scales.rearrange("s f t -> f s t"), nc.scalar)
+        xsp = keep.tile([P, T], U8, name="xsp", tag="xsp", align_bytes=64)
+        nc.vector.memset(xsp[:].bitcast(I32), 0)
+        nc.scalar.dma_start(xsp[:16 * PASSES].bitcast(I32), x_scales.rearrange("s f t -> f s t").bitcast(I32))
         late = stage(0)
-        load_w1(late, 6, 7)
-        zero_scales(6, 7)
-        load_w1s(6, 7, 0)
-        load_w1(late, 0, 1)
-        load_w1(late, 1, 2)
+        xb = late.tile([P, PASSES - 1, T], I32, name="xb", align_bytes=64)
+        nc.sync.dma_start(xb[:], x_rows[:, 1:, :])
+        xw = [xa[:]] + [xb[:, s, :] for s in range(PASSES - 1)]
+        clear_window(0)
+        load_w1s(keep, nc.vector, 0, FIRST)
+
         late = stage(1)
-        zero_scales(0, 3)
-        load_w1s(0, 3, 0)
-        load_w1(late, 2, 3)
-        load_w1(late, 3, 4)
-        load_gate(late, 1, 3)
+        w1b = late.tile([P, PASSES, 2 * H], U8, name="w1b", tag="w1b", align_bytes=64)
+        load_w1(w1b, 1, 1)
+        load_w2(late, "w2a", 0, 3)
+        w1c = late.tile([P, PASSES, 2 * H], U8, name="w1c", align_bytes=64)
+        load_w1(w1c, 2, 2)
+        load_gate(late, "gatea", 0, 3)
+        w2s = late.tile([P, E + 1, N], U8, name="w2s", align_bytes=64)
         nc.vector.memset(w2s[:].bitcast(I32), 0)
-        load_w2s(0)
-        load_w2(late, 0, 3)
-        zero_scales(3, 6)
-        load_w1s(3, 6, 0)
-        load_gate(late, 0, 1)
+        load_scales(w2s, w2_scales.rearrange("e s f n -> f (e s) n"))
+        first_late = late
         late = stage(2)
-        load_w1(late, 5, 6)
-        load_w1(late, 4, 5)
-        load_w2(late, 3, 7)
-        load_gate(late, 3, 6)
+        w1d = late.tile([P, PASSES, 2 * H], U8, name="w1d", align_bytes=64)
+        load_w1(w1d, E, E)
+        gs_late = late.tile([P, PASSES, S - EARLY * C], U8, name="gs_late", align_bytes=64)
+        nc.gpsimd.memset(gs_late[:].bitcast(I32), 0)
+        load_w1s(late, nc.gpsimd, FIRST, E + 1)
+        ident = late.tile([P, P], F32, name="ident")
         make_identity(nc, ident[:])
+        clear_window(1)
+        clear_window(2)
 
-        for n in range(NT):
-            nc.scalar.activation(windows[n][:], zero[:, 8 * n:8 * n + 1].to_broadcast([P, T]), SILU)
-
-        def group_offsets(g):
-            e0, e1 = GROUPS[g]
-            return offsets[:, e0 * C // 16:e1 * C // 16]
-
+        gs_early = keep.tile([P, PASSES, EARLY * C], U8, name="gs_early", align_bytes=64)
         for s in range(PASSES):
-            nc.vector.tensor_copy(gw[:, s, :], xw[s][:].bitcast(U32).indirect(offsets[:]))
+            nc.vector.tensor_copy(gs_early[:, s, :], xs[:, s, :].indirect(slots(0, EARLY)))
+        gw = {}
 
-        gs = {}
+        def gather_words(e0, e1, s0, s1, tag):
+            t = keep.tile([P, s1 - s0, (e1 - e0) * C], U32, name="gw%d_%d" % (e0, s0), tag=tag, align_bytes=64)
+            for s in range(s0, s1):
+                nc.vector.tensor_copy(t[:, s - s0, :], xw[s].bitcast(U32).indirect(slots(e0, e1)))
+                for e in range(e0, e1):
+                    gw[e, s] = t[:, s - s0, (e - e0) * C:(e - e0 + 1) * C]
 
-        def gather(g, tag=""):
-            e0, e1 = GROUPS[g]
-            gs[g] = keep.tile([P, PASSES, (e1 - e0) * C], U8, name="gs%d" % g, tag=tag or "gs%d" % g, align_bytes=64)
+        hw = keep.tile([P, S + T], U32, name="hw", align_bytes=64)
+        hs = keep.tile([P, S + T], U8, name="hs", align_bytes=64)
+        hb, ysb = {}, {}
+        count = []
+
+        def layer1(i):
+            a = bank(len(count) % 3)
+            count.append(i)
             for s in range(PASSES):
-                nc.vector.tensor_copy(gs[g][:, s, :], xs[:, s, :].indirect(group_offsets(g)))
-
-        hb = {}
-
-        def layer1(i, b):
-            a = bank(b)
-            for s in range(PASSES):
-                if i < E:
-                    e = i
-                    g = [j for j in range(len(GROUPS)) if GROUPS[j][0] <= e < GROUPS[j][1]][0]
-                    c0 = (e - GROUPS[g][0]) * C
-                    words, scales = gw[:, s, e * C:(e + 1) * C], gs[g][:, s, c0:c0 + C]
+                if i < EARLY:
+                    e, words, scales = i, gw[i, s], gs_early[:, s, i * C:(i + 1) * C]
+                elif i < E:
+                    e, words, scales = i, gw[i, s], gs_late[:, s, (i - EARLY) * C:(i - EARLY + 1) * C]
                 else:
-                    e = E
                     t0 = (i - E) * P
-                    words, scales = xw[s][:, t0:t0 + P], xs[:, s, t0:t0 + P]
+                    e, words, scales = E, xw[s][:, t0:t0 + P], xs[:, s, t0:t0 + P]
                 nc.tensor.matmul_mx(
                     out=a[:], lhsT=words.bitcast(FP8X4), lhsT_scale=scales,
-                    rhs=w1w[e, s].bitcast(FP4X4), rhs_scale=w1s[:, e * PASSES + s, :],
+                    rhs=w1w[e, s].bitcast(FP4X4), rhs_scale=w1s[e, s],
                     start=(s == 0), stop=(s == PASSES - 1))
             h = keep.tile([P, 2, P, 2], BF16, name="h%d" % i, tag="h%d" % i)
             nc.scalar.activation(h[:], a[:].rearrange("t (p u e) -> t u p e", u=2, e=2), SILU)
@@ -192,82 +182,95 @@ def tile_moe_shr_mlp_silu_kernel(tc, x_words, x_scales, w1_words, w1_scales, w2_
                 lhsT_scale=w2s[:, e, n * P:(n + 1) * P],
                 rhs=hw[:, cols].bitcast(FP8X4), rhs_scale=hs[:, cols], start=True, stop=True)
 
-        def routed2(e, b):
+        def routed2(e, n0, n1, b):
             y = bank(b)
-            for n in range(NT):
+            for n in range(n0, n1):
                 layer2(y[:, n * P:(n + 1) * P], e, n, slice(e * C, (e + 1) * C))
-            g = [j for j in range(len(SGROUPS)) if SGROUPS[j][0] <= e < SGROUPS[j][1]][0]
-            c0 = (e - SGROUPS[g][0]) * C
-            nc.scalar.copy(ysb[g][:, :, c0:c0 + C], y[:, :N].rearrange("p (n j) -> p n j", n=NT))
+            t = keep.tile([P, (n1 - n0) * C], F32, name="y%d_%d" % (e, n0))
+            nc.scalar.copy(t[:], y[:, n0 * P:n1 * P])
+            for n in range(n0, n1):
+                ysb[e, n] = t[:, (n - n0) * C:(n - n0 + 1) * C]
 
-        def scatter(g, n):
-            e0, e1 = SGROUPS[g]
-            tile, first = gates[e0]
-            nc.vector.tensor_tensor(windows[n][:].indirect(offsets[:, e0 * C // 16:e1 * C // 16]),
-                                    ysb[g][:, n, :], tile[:, n, (e0 - first) * C:(e1 - first) * C], MULT)
+        def scatter(e, n):
+            nc.vector.tensor_tensor(windows[n][:].indirect(slots(e, e + 1)), ysb[e, n], gates[e], MULT)
 
-        def finish(n, t0, t1, b):
+        def put_back(e, b):
+            routed2(e, 0, NT, b)
+            for n in range(NT):
+                scatter(e, n)
+
+        ys = {}
+
+        def shared2(n, half, b):
             y = bank(b)
-            layer2(y[:, :t1 - t0], E, n, slice(S + t0, S + t1))
-            res = keep.tile([P, t1 - t0], F32, name="res%d_%d" % (n, t0))
-            nc.vector.tensor_tensor(res[:], y[:, :t1 - t0], windows[n][:, t0:t1], ADD)
-            nc.sync.dma_start(out[n * P:(n + 1) * P, t0:t1], res[:])
+            layer2(y[:], E, n, slice(S + half * BANK, S + (half + 1) * BANK))
+            ys[n, half] = y
 
-        gather(0)
-        layer1(8, 7)
-        layer1(6, 3)
-        layer1(7, 4)
-        gather(1)
-        turn(6, 8, 5)
-        layer1(1, 4)
-        layer1(0, 2)
-        layer1(9, 3)
-        turn(1, 2, 5)
-        turn(0, 1, 2)
-        routed2(0, 1)
-        gather(2)
-        layer1(2, 6)
-        routed2(1, 2)
-        turn(2, 3, 4)
-        scatter(1, 1)
-        layer1(3, 6)
-        turn(3, 4, 3)
-        layer1(13, 0)
-        scatter(0, 2)
-        turn(8, 10, 5)
-        layer1(10, 2)
-        gather(3)
-        scatter(1, 0)
-        routed2(2, 3)
+        def finish(n, half):
+            cols = slice(half * BANK, (half + 1) * BANK)
+            res = keep.tile([P, BANK], F32, name="res%d_%d" % (n, half))
+            nc.vector.tensor_tensor(res[:], ys[n, half][:], windows[n][:, cols], ADD)
+            nc.sync.dma_start(out[n * P:(n + 1) * P, cols], res[:])
+
+        gather_words(0, 4, 0, 1, "gw_first")
+        gather_words(0, 1, 1, PASSES, "gw0")
+        gather_words(1, 2, 1, PASSES, "gw1")
+        gather_words(2, 4, 1, PASSES, "gw2")
+        warm = bank(7)
+        for i in range(WARM):
+            nc.tensor.matmul_mx(out=warm[:], lhsT=xw[0][:, :P].bitcast(FP8X4), lhsT_scale=xs[:, 0, :P],
+                                rhs=w1w[0, 0].bitcast(FP4X4), rhs_scale=xs[:, 0, :H], start=True, stop=True)
+        layer1(0)
+        gs_packed = keep.tile([P, S - EARLY * C], U8, name="gs_packed", tag="gw0", align_bytes=64)
+        nc.vector.tensor_copy(gs_packed[:], xsp[:].indirect(slots(EARLY, E)))
+        for q in (0, 2, 1, 3):
+            nc.sync.dma_start(gs_late[32 * q:32 * q + 4].bitcast(I32),
+                                gs_packed[4 * PASSES * q:4 * PASSES * (q + 1)].bitcast(I32))
+
+        w1e = keep.tile([P, (E - FIRST) * PASSES, 2 * H], U8, name="w1e", tag="xsp", align_bytes=64)
+        for e in range(FIRST, E):
+            load_w1(w1e, FIRST, e)
+
+        load_w2(keep, "w1a", 3, E + 1)
+        layer1(1)
+        load_gate(first_late, "w1b", 3, E)
+        turn(0, 1, 3)
+        gather_words(4, 6, 0, PASSES, "grouped0")
+        routed2(0, 0, 1, 3)
         scatter(0, 0)
+        turn(1, 2, 4)
+        routed2(0, 1, NT, 4)
         scatter(0, 1)
-        layer1(11, 1)
-        layer1(5, 0)
-        scatter(1, 2)
-        layer1(4, 6)
-        scatter(2, 0)
-        turn(5, 6, 1)
-        routed2(3, 7)
-        scatter(2, 1)
-        scatter(2, 2)
-        turn(10, 12, 5)
-        turn(4, 5, 2)
-        routed2(5, 5)
-        scatter(3, 0)
-        scatter(3, 2)
-        layer1(12, 7)
-        scatter(3, 1)
-        routed2(4, 1)
-        scatter(5, 2)
-        scatter(5, 0)
-        turn(12, 14, 0)
-        scatter(5, 1)
-        scatter(4, 2)
-        scatter(4, 0)
-        finish(2, 512, 1024, 6)
-        finish(2, 0, 512, 2)
-        scatter(4, 1)
-        finish(0, 0, 512, 7)
-        finish(1, 0, 512, 1)
-        finish(0, 512, 1024, 0)
-        finish(1, 512, 1024, 3)
+        scatter(0, 2)
+        layer1(2)
+        turn(2, 3, 3)
+        put_back(1, 3)
+        layer1(6)
+        layer1(7)
+        turn(6, 8, 5)
+        layer1(3)
+        turn(3, 4, 4)
+        put_back(2, 4)
+        layer1(8)
+        layer1(9)
+        turn(8, 10, 6)
+        layer1(4)
+        turn(4, 5, 3)
+        put_back(3, 3)
+        layer1(5)
+        turn(5, 6, 4)
+        put_back(4, 4)
+        layer1(10)
+        layer1(11)
+        turn(10, 12, 7)
+        layer1(12)
+        layer1(13)
+        turn(12, 14, 5)
+        routed2(5, 0, NT, 5)
+        for n in range(NT):
+            shared2(n, 0, (6, 7, 0)[n])
+            shared2(n, 1, (3, 1, 2)[n])
+        for n in range(NT):
+            scatter(5, n)
+            finish(n, 0)
+            finish(n, 1)

@@ -25,7 +25,6 @@ S = E * C
 BANK = 512
 FIRST = 3
 WARM = 6
-EARLY = 3
 
 
 def tile_moe_shr_mlp_silu_kernel(tc, x_words, x_scales, w1_words, w1_scales, w2_words, w2_scales, gate, offs, out):
@@ -53,9 +52,9 @@ def tile_moe_shr_mlp_silu_kernel(tc, x_words, x_scales, w1_words, w1_scales, w2_
                 nc.vector.tensor_copy(zero[:, 8 * n:8 * n + 1], staged[:])
             return ctx.enter_context(tc.tile_pool(name="late%d" % n, bufs=1))
 
-        def load_scales(plane, rows, queue=nc.sync):
-            for q in (0, 2, 1, 3):
-                queue.dma_start(plane[32 * q:32 * q + 4].bitcast(I32), rows[4 * q:4 * q + 4].bitcast(I32))
+        def load_scales(plane, rows):
+            for r in range(4):
+                nc.sync.dma_start(plane[r:P:32].bitcast(I32), rows[r:16:4].bitcast(I32))
 
         w1w, w1s, w2w, gates = {}, {}, {}, {}
 
@@ -65,9 +64,9 @@ def tile_moe_shr_mlp_silu_kernel(tc, x_words, x_scales, w1_words, w1_scales, w2_
             for s in range(PASSES):
                 w1w[e, s] = tile[:, (e - first) * PASSES + s, :]
 
-        def load_w1s(pool, engine, e0, e1):
+        def load_w1s(pool, e0, e1):
             t = pool.tile([P, (e1 - e0) * PASSES, H], U8, name="w1s%d" % e0, align_bytes=64)
-            engine.memset(t[:].bitcast(I32), 0)
+            nc.vector.memset(t[:].bitcast(I32), 0)
             load_scales(t, w1_scales[e0:e1].rearrange("e s f i -> f (e s) i"))
             for e in range(e0, e1):
                 for s in range(PASSES):
@@ -94,42 +93,45 @@ def tile_moe_shr_mlp_silu_kernel(tc, x_words, x_scales, w1_words, w1_scales, w2_
         nc.sync.dma_start(xa[:], x_rows[:, 0, :])
         xs = keep.tile([P, PASSES, T], U8, name="xs", align_bytes=64)
         nc.vector.memset(xs[:].bitcast(I32), 0)
-        load_scales(xs, x_scales.rearrange("s f t -> f s t"), nc.scalar)
-        xsp = keep.tile([P, T], U8, name="xsp", tag="xsp", align_bytes=64)
-        nc.vector.memset(xsp[:].bitcast(I32), 0)
-        nc.scalar.dma_start(xsp[:16 * PASSES].bitcast(I32), x_scales.rearrange("s f t -> f s t").bitcast(I32))
+        load_scales(xs, x_scales.rearrange("s f t -> f s t"))
+
         late = stage(0)
         xb = late.tile([P, PASSES - 1, T], I32, name="xb", align_bytes=64)
         nc.sync.dma_start(xb[:], x_rows[:, 1:, :])
         xw = [xa[:]] + [xb[:, s, :] for s in range(PASSES - 1)]
         clear_window(0)
-        load_w1s(keep, nc.vector, 0, FIRST)
-
-        late = stage(1)
-        w1b = late.tile([P, PASSES, 2 * H], U8, name="w1b", tag="w1b", align_bytes=64)
-        load_w1(w1b, 1, 1)
-        load_w2(late, "w2a", 0, 3)
-        w1c = late.tile([P, PASSES, 2 * H], U8, name="w1c", align_bytes=64)
-        load_w1(w1c, 2, 2)
-        load_gate(late, "gatea", 0, 3)
-        w2s = late.tile([P, E + 1, N], U8, name="w2s", align_bytes=64)
+        load_w1s(keep, 0, FIRST)
+        w2s = keep.tile([P, E + 1, N], U8, name="w2s", align_bytes=64)
         nc.vector.memset(w2s[:].bitcast(I32), 0)
         load_scales(w2s, w2_scales.rearrange("e s f n -> f (e s) n"))
-        first_late = late
+
+        first_late = late = stage(1)
+        w1b = late.tile([P, PASSES, 2 * H], U8, name="w1b", tag="w1b", align_bytes=64)
+        load_w1(w1b, 1, 1)
+        load_w2(late, "w2a", 0, 4)
+        load_gate(late, "gatea", 0, 3)
+        w1c = late.tile([P, PASSES, 2 * H], U8, name="w1c", align_bytes=64)
+        load_w1(w1c, 2, 2)
+        clear_window(1)
+        load_w1s(keep, FIRST, E + 1)
+
         late = stage(2)
-        w1d = late.tile([P, PASSES, 2 * H], U8, name="w1d", align_bytes=64)
-        load_w1(w1d, E, E)
-        gs_late = late.tile([P, PASSES, S - EARLY * C], U8, name="gs_late", align_bytes=64)
-        nc.gpsimd.memset(gs_late[:].bitcast(I32), 0)
-        load_w1s(late, nc.gpsimd, FIRST, E + 1)
+        w1d = late.tile([P, (E + 1 - FIRST) * PASSES, 2 * H], U8, name="w1d", align_bytes=64)
+        for e in (3, 6, 4, 5):
+            load_w1(w1d, FIRST, e)
         ident = late.tile([P, P], F32, name="ident")
         make_identity(nc, ident[:])
-        clear_window(1)
         clear_window(2)
 
-        gs_early = keep.tile([P, PASSES, EARLY * C], U8, name="gs_early", align_bytes=64)
-        for s in range(PASSES):
-            nc.vector.tensor_copy(gs_early[:, s, :], xs[:, s, :].indirect(slots(0, EARLY)))
+        gs = {}
+
+        def gather_scales(e0, e1, tag):
+            t = keep.tile([P, PASSES, (e1 - e0) * C], U8, name="gs%d" % e0, tag=tag, align_bytes=64)
+            for s in range(PASSES):
+                nc.vector.tensor_copy(t[:, s, :], xs[:, s, :].indirect(slots(e0, e1)))
+                for e in range(e0, e1):
+                    gs[e, s] = t[:, s, (e - e0) * C:(e - e0 + 1) * C]
+
         gw = {}
 
         def gather_words(e0, e1, s0, s1, tag):
@@ -148,10 +150,8 @@ def tile_moe_shr_mlp_silu_kernel(tc, x_words, x_scales, w1_words, w1_scales, w2_
             a = bank(len(count) % 3)
             count.append(i)
             for s in range(PASSES):
-                if i < EARLY:
-                    e, words, scales = i, gw[i, s], gs_early[:, s, i * C:(i + 1) * C]
-                elif i < E:
-                    e, words, scales = i, gw[i, s], gs_late[:, s, (i - EARLY) * C:(i - EARLY + 1) * C]
+                if i < E:
+                    e, words, scales = i, gw[i, s], gs[i, s]
                 else:
                     t0 = (i - E) * P
                     e, words, scales = E, xw[s][:, t0:t0 + P], xs[:, s, t0:t0 + P]
@@ -212,33 +212,26 @@ def tile_moe_shr_mlp_silu_kernel(tc, x_words, x_scales, w1_words, w1_scales, w2_
             nc.vector.tensor_tensor(res[:], ys[n, half][:], windows[n][:, cols], ADD)
             nc.sync.dma_start(out[n * P:(n + 1) * P, cols], res[:])
 
-        gather_words(0, 4, 0, 1, "gw_first")
+        gather_words(0, E, 0, 1, "gw_first")
+        gather_scales(0, 3, "gs0")
         gather_words(0, 1, 1, PASSES, "gw0")
         gather_words(1, 2, 1, PASSES, "gw1")
         gather_words(2, 4, 1, PASSES, "gw2")
+        gather_words(4, E, 1, PASSES, "gw4")
         warm = bank(7)
         for i in range(WARM):
             nc.tensor.matmul_mx(out=warm[:], lhsT=xw[0][:, :P].bitcast(FP8X4), lhsT_scale=xs[:, 0, :P],
                                 rhs=w1w[0, 0].bitcast(FP4X4), rhs_scale=xs[:, 0, :H], start=True, stop=True)
         layer1(0)
-        gs_packed = keep.tile([P, S - EARLY * C], U8, name="gs_packed", tag="gw0", align_bytes=64)
-        nc.vector.tensor_copy(gs_packed[:], xsp[:].indirect(slots(EARLY, E)))
-        for q in (0, 2, 1, 3):
-            nc.sync.dma_start(gs_late[32 * q:32 * q + 4].bitcast(I32),
-                                gs_packed[4 * PASSES * q:4 * PASSES * (q + 1)].bitcast(I32))
-
-        w1e = keep.tile([P, (E - FIRST) * PASSES, 2 * H], U8, name="w1e", tag="xsp", align_bytes=64)
-        for e in range(FIRST, E):
-            load_w1(w1e, FIRST, e)
-
-        load_w2(keep, "w1a", 3, E + 1)
+        load_w2(keep, "w1a", 4, E + 1)
         layer1(1)
         load_gate(first_late, "w1b", 3, E)
         turn(0, 1, 3)
-        gather_words(4, 6, 0, PASSES, "grouped0")
+        gather_scales(3, 4, "grouped0")
         routed2(0, 0, 1, 3)
         scatter(0, 0)
         turn(1, 2, 4)
+        gather_scales(4, E, "grouped1")
         routed2(0, 1, NT, 4)
         scatter(0, 1)
         scatter(0, 2)
@@ -257,20 +250,20 @@ def tile_moe_shr_mlp_silu_kernel(tc, x_words, x_scales, w1_words, w1_scales, w2_
         layer1(4)
         turn(4, 5, 3)
         put_back(3, 3)
-        layer1(5)
-        turn(5, 6, 4)
-        put_back(4, 4)
         layer1(10)
         layer1(11)
         turn(10, 12, 7)
+        layer1(5)
+        turn(5, 6, 4)
+        put_back(4, 4)
         layer1(12)
         layer1(13)
+        routed2(5, 0, NT, 3)
         turn(12, 14, 5)
-        routed2(5, 0, NT, 5)
         for n in range(NT):
-            shared2(n, 0, (6, 7, 0)[n])
-            shared2(n, 1, (3, 1, 2)[n])
-        for n in range(NT):
+            shared2(n, 0, (6, 7, 4)[n])
             scatter(5, n)
             finish(n, 0)
+        for n in range(NT):
+            shared2(n, 1, n)
             finish(n, 1)

@@ -23,8 +23,10 @@ PASSES = K // 512
 NT = N // P
 S = E * C
 BANK = 512
-FIRST = 3
+FIRST = 4
+EARLY = 1
 WARM = 6
+LAST = 64
 
 
 def tile_moe_shr_mlp_silu_kernel(tc, x_words, x_scales, w1_words, w1_scales, w2_words, w2_scales, gate, offs, out):
@@ -52,129 +54,161 @@ def tile_moe_shr_mlp_silu_kernel(tc, x_words, x_scales, w1_words, w1_scales, w2_
                 nc.vector.tensor_copy(zero[:, 8 * n:8 * n + 1], staged[:])
             return ctx.enter_context(tc.tile_pool(name="late%d" % n, bufs=1))
 
-        def load_scales(plane, rows):
+        def planes(name, count, width):
+            return keep.tile([P, count, width], U8, name=name, align_bytes=64)
+
+        def clear(tile, b0, b1):
+            nc.vector.memset(tile[:].rearrange("p a w -> p (a w)")[:, b0:b1].bitcast(I32), 0)
+
+        def load_scales(tile, rows):
             for r in range(4):
-                nc.sync.dma_start(plane[r:P:32].bitcast(I32), rows[r:16:4].bitcast(I32))
+                nc.sync.dma_start(tile[r:P:32].bitcast(I32), rows[r:16:4].bitcast(I32))
 
-        w1w, w1s, w2w, gates = {}, {}, {}, {}
+        w1w, w2w, gates = {}, {}, {}
 
-        def load_w1(tile, first, e):
-            rows = tile[:, (e - first) * PASSES:(e - first + 1) * PASSES, :]
-            nc.sync.dma_start(rows.bitcast(I32), w1_words[e].rearrange("s p b -> p s b").bitcast(I32))
-            for s in range(PASSES):
-                w1w[e, s] = tile[:, (e - first) * PASSES + s, :]
+        def load_w1(pool, e):
+            t = pool.tile([P, PASSES, 2 * H], U8, name="w1w%d" % e, align_bytes=64)
+            nc.sync.dma_start(t[:].bitcast(I32), w1_words[e].rearrange("s p b -> p s b").bitcast(I32))
+            w1w[e] = t
 
-        def load_w1s(pool, e0, e1):
-            t = pool.tile([P, (e1 - e0) * PASSES, H], U8, name="w1s%d" % e0, align_bytes=64)
-            nc.vector.memset(t[:].bitcast(I32), 0)
-            load_scales(t, w1_scales[e0:e1].rearrange("e s f i -> f (e s) i"))
-            for e in range(e0, e1):
-                for s in range(PASSES):
-                    w1s[e, s] = t[:, (e - e0) * PASSES + s, :]
-
-        def load_w2(pool, tag, e0, e1):
-            t = pool.tile([P, e1 - e0, 2 * N], U8, name="w2w%d" % e0, tag=tag, align_bytes=64)
+        def load_w2(pool, e0, e1):
+            t = pool.tile([P, e1 - e0, 2 * N], U8, name="w2w%d" % e0, align_bytes=64)
             nc.sync.dma_start(t[:].bitcast(I32), w2_words[e0:e1].rearrange("e s p b -> p (e s) b").bitcast(I32))
             for e in range(e0, e1):
                 w2w[e] = t[:, e - e0, :]
 
-        def load_gate(pool, tag, e0, e1):
-            g = pool.tile([P, (e1 - e0) * C], F32, name="gate%d" % e0, tag=tag, align_bytes=64)
+        def load_gate(pool, e0, e1):
+            g = pool.tile([P, (e1 - e0) * C], F32, name="gate%d" % e0)
             nc.sync.dma_start(g[:], gate[:P, e0 * C:e1 * C])
             for e in range(e0, e1):
-                gates[e] = g[:, (e - e0) * C:(e - e0 + 1) * C]
+                gates[e] = (g, e0)
+
+        x_rows = x_words.rearrange("s p t r -> p s (t r)").bitcast(I32)
+        x_planes = x_scales.rearrange("s f t -> f s t")
+        w1_planes = w1_scales.rearrange("e s f i -> f (e s) i")
+        xs = planes("xs", PASSES, T)
+        w1s_first = planes("w1s_first", FIRST * PASSES, H)
+        w1s_rest = planes("w1s_rest", (E + 1 - FIRST) * PASSES, H)
+        w2s = planes("w2s", E + 1, N)
+        gs_moved = planes("gs_moved", PASSES - 1, S - EARLY * C)
 
         offsets = keep.tile([P, S // 16], U16, name="offsets")
         nc.sync.dma_start(offsets[:], offs)
-        w1a = keep.tile([P, PASSES, 2 * H], U8, name="w1a", tag="w1a", align_bytes=64)
-        load_w1(w1a, 0, 0)
-        x_rows = x_words.rearrange("s p t r -> p s (t r)").bitcast(I32)
+        load_w1(keep, 0)
         xa = keep.tile([P, T], I32, name="xa", align_bytes=64)
         nc.sync.dma_start(xa[:], x_rows[:, 0, :])
-        xs = keep.tile([P, PASSES, T], U8, name="xs", align_bytes=64)
-        nc.vector.memset(xs[:].bitcast(I32), 0)
-        load_scales(xs, x_scales.rearrange("s f t -> f s t"))
+        clear(xs, 0, PASSES * T)
+        for half in range(2):
+            nc.sync.dma_start(xs[64 * half + 4:64 * half + 20, 0, :].bitcast(I32),
+                              x_planes[8 * half:8 * half + 8, 1:, :].bitcast(I32))
+        load_scales(xs, x_planes)
 
         late = stage(0)
         xb = late.tile([P, PASSES - 1, T], I32, name="xb", align_bytes=64)
         nc.sync.dma_start(xb[:], x_rows[:, 1:, :])
         xw = [xa[:]] + [xb[:, s, :] for s in range(PASSES - 1)]
         clear_window(0)
-        load_w1s(keep, 0, FIRST)
-        w2s = keep.tile([P, E + 1, N], U8, name="w2s", align_bytes=64)
-        nc.vector.memset(w2s[:].bitcast(I32), 0)
-        load_scales(w2s, w2_scales.rearrange("e s f n -> f (e s) n"))
+        clear(w1s_first, 0, FIRST * PASSES * H)
+        load_scales(w1s_first, w1_planes[:, :FIRST * PASSES, :])
 
-        first_late = late = stage(1)
-        w1b = late.tile([P, PASSES, 2 * H], U8, name="w1b", tag="w1b", align_bytes=64)
-        load_w1(w1b, 1, 1)
-        load_w2(late, "w2a", 0, 4)
-        load_gate(late, "gatea", 0, 3)
-        w1c = late.tile([P, PASSES, 2 * H], U8, name="w1c", align_bytes=64)
-        load_w1(w1c, 2, 2)
-        clear_window(1)
-        load_w1s(keep, FIRST, E + 1)
-
-        late = stage(2)
-        w1d = late.tile([P, (E + 1 - FIRST) * PASSES, 2 * H], U8, name="w1d", align_bytes=64)
-        for e in (3, 6, 4, 5):
-            load_w1(w1d, FIRST, e)
+        late = stage(1)
+        load_w1(late, 1)
         ident = late.tile([P, P], F32, name="ident")
         make_identity(nc, ident[:])
-        clear_window(2)
+        clear_window(1)
+        clear(gs_moved, 0, (PASSES - 1) * (S - EARLY * C))
+        clear(w2s, LAST, (E + 1) * N)
+        clear(w1s_rest, LAST, (E + 1 - FIRST) * PASSES * H)
 
-        gs = {}
+        gw, gs = {}, {}
 
-        def gather_scales(e0, e1, tag):
-            t = keep.tile([P, PASSES, (e1 - e0) * C], U8, name="gs%d" % e0, tag=tag, align_bytes=64)
-            for s in range(PASSES):
-                nc.vector.tensor_copy(t[:, s, :], xs[:, s, :].indirect(slots(e0, e1)))
-                for e in range(e0, e1):
-                    gs[e, s] = t[:, s, (e - e0) * C:(e - e0 + 1) * C]
-
-        gw = {}
-
-        def gather_words(e0, e1, s0, s1, tag):
-            t = keep.tile([P, s1 - s0, (e1 - e0) * C], U32, name="gw%d_%d" % (e0, s0), tag=tag, align_bytes=64)
+        def gather_words(e0, e1, s0, s1):
+            t = keep.tile([P, s1 - s0, (e1 - e0) * C], U32, name="gw%d_%d" % (e0, s0), align_bytes=64)
             for s in range(s0, s1):
                 nc.vector.tensor_copy(t[:, s - s0, :], xw[s].bitcast(U32).indirect(slots(e0, e1)))
                 for e in range(e0, e1):
                     gw[e, s] = t[:, s - s0, (e - e0) * C:(e - e0 + 1) * C]
 
+        gather_words(0, E, 0, 1)
+        gs_packed = keep.tile([P, S - EARLY * C], U8, name="gs_packed", align_bytes=64)
+        nc.vector.tensor_copy(gs_packed[:], xs[:, 0, :].indirect(slots(EARLY, E)))
+        for q in (0, 2, 1, 3):
+            first = 64 * (q // 2) + 4 + 8 * (q % 2)
+            nc.scalar.dma_start(gs_moved[32 * q:32 * q + 4].bitcast(I32), gs_packed[first:first + 8].bitcast(I32))
+        for e in range(EARLY, E):
+            cols = slice((e - EARLY) * C, (e - EARLY + 1) * C)
+            gs[e, 0] = gs_packed[:, cols]
+            for s in range(1, PASSES):
+                gs[e, s] = gs_moved[:, s - 1, cols]
+
+        late = stage(2)
+        load_w2(late, 0, 4)
+        load_gate(late, 0, 2)
+        clear(w2s, 0, LAST)
+        load_scales(w2s, w2_scales.rearrange("e s f n -> f (e s) n"))
+        load_w1(late, 2)
+        load_w1(late, 3)
+        load_gate(late, 2, E)
+        clear(w1s_rest, 0, LAST)
+        load_scales(w1s_rest, w1_planes[:, FIRST * PASSES:, :])
+        for e in (E, 4, 5):
+            load_w1(late, e)
+        load_w2(late, 4, E + 1)
+        clear_window(2)
+        gs_early = planes("gs_early", PASSES, EARLY * C)
+        for s in range(PASSES):
+            nc.vector.tensor_copy(gs_early[:, s, :], xs[:, s, :].indirect(slots(0, EARLY)))
+            for e in range(EARLY):
+                gs[e, s] = gs_early[:, s, e * C:(e + 1) * C]
+        gather_words(0, 2, 1, PASSES)
+        gather_words(2, E, 1, PASSES)
+
         hw = keep.tile([P, S + T], U32, name="hw", align_bytes=64)
         hs = keep.tile([P, S + T], U8, name="hs", align_bytes=64)
-        hb, ysb = {}, {}
-        count = []
+        hb, ysb, ys = {}, {}, {}
 
-        def layer1(i):
-            a = bank(len(count) % 3)
-            count.append(i)
+        def layer1(i, b):
+            a = bank(b)
+            e = min(i, E)
             for s in range(PASSES):
                 if i < E:
-                    e, words, scales = i, gw[i, s], gs[i, s]
+                    words, scales = gw[i, s], gs[i, s]
                 else:
                     t0 = (i - E) * P
-                    e, words, scales = E, xw[s][:, t0:t0 + P], xs[:, s, t0:t0 + P]
+                    words, scales = xw[s][:, t0:t0 + P], xs[:, s, t0:t0 + P]
+                if e < FIRST:
+                    w_scales = w1s_first[:, e * PASSES + s, :]
+                else:
+                    w_scales = w1s_rest[:, (e - FIRST) * PASSES + s, :]
                 nc.tensor.matmul_mx(
                     out=a[:], lhsT=words.bitcast(FP8X4), lhsT_scale=scales,
-                    rhs=w1w[e, s].bitcast(FP4X4), rhs_scale=w1s[e, s],
+                    rhs=w1w[e][:, s, :].bitcast(FP4X4), rhs_scale=w_scales,
                     start=(s == 0), stop=(s == PASSES - 1))
-            h = keep.tile([P, 2, P, 2], BF16, name="h%d" % i, tag="h%d" % i)
+            h = keep.tile([P, 2, P, 2], BF16, name="h%d" % i)
             nc.scalar.activation(h[:], a[:].rearrange("t (p u e) -> t u p e", u=2, e=2), SILU)
             hb[i] = h
 
-        def turn(i0, i1, b):
+        def grouped(i0, i1):
+            return keep.tile([P, (i1 - i0) * H], BF16, name="grouped%d" % i0, align_bytes=64)
+
+        def turn(i0, i1, b, dst):
             k = i1 - i0
             tr = bank(b)[:].rearrange("p (h w t) -> p h w t", h=2, w=2)
             for i in range(i0, i1):
                 words = hb[i][:].rearrange("t u p e -> t (u p e)").bitcast(F32)
                 for w in range(2):
                     nc.tensor.transpose(tr[:, i - i0, w, :], words[:, w * P:(w + 1) * P], ident[:])
-            grouped = keep.tile([P, 4 * P * k], BF16, name="grouped%d" % i0, tag="grouped%d" % i0, align_bytes=64)
-            nc.scalar.copy(grouped[:].bitcast(F32).rearrange("p (h t w) -> p h t w", h=k, w=2),
+            nc.scalar.copy(dst.bitcast(F32).rearrange("p (h t w) -> p h t w", h=k, w=2),
                            tr[:, :k, :, :].rearrange("p h w t -> p h t w"))
+
+        def quantise(i0, i1, src):
             cols = slice(i0 * P, i1 * P)
-            nc.vector.quantize_mx(out=hw[:, cols].bitcast(FP8X4), scales=hs[:, cols], in_=grouped[:])
+            nc.vector.quantize_mx(out=hw[:, cols].bitcast(FP8X4), scales=hs[:, cols], in_=src)
+
+        def turn_routed(e0, e1, b):
+            g = grouped(e0, e1)
+            turn(e0, e1, b, g[:])
+            quantise(e0, e1, g[:])
 
         def layer2(dst, e, n, cols):
             nc.tensor.matmul_mx(
@@ -182,88 +216,62 @@ def tile_moe_shr_mlp_silu_kernel(tc, x_words, x_scales, w1_words, w1_scales, w2_
                 lhsT_scale=w2s[:, e, n * P:(n + 1) * P],
                 rhs=hw[:, cols].bitcast(FP8X4), rhs_scale=hs[:, cols], start=True, stop=True)
 
-        def routed2(e, n0, n1, b):
+        def put_back(e0, e1, n0, n1, b):
             y = bank(b)
+            width = (e1 - e0) * C
             for n in range(n0, n1):
-                layer2(y[:, n * P:(n + 1) * P], e, n, slice(e * C, (e + 1) * C))
-            t = keep.tile([P, (n1 - n0) * C], F32, name="y%d_%d" % (e, n0))
-            nc.scalar.copy(t[:], y[:, n0 * P:n1 * P])
+                for e in range(e0, e1):
+                    c0 = (n - n0) * width + (e - e0) * C
+                    layer2(y[:, c0:c0 + C], e, n, slice(e * C, (e + 1) * C))
+            t = keep.tile([P, (n1 - n0) * width], F32, name="y%d_%d" % (e0, n0))
+            nc.scalar.copy(t[:], y[:, :(n1 - n0) * width])
+            g, first = gates[e0]
             for n in range(n0, n1):
-                ysb[e, n] = t[:, (n - n0) * C:(n - n0 + 1) * C]
+                ysb[e0, n] = t[:, (n - n0) * width:(n - n0 + 1) * width]
+                nc.vector.tensor_tensor(windows[n][:].indirect(slots(e0, e1)), ysb[e0, n],
+                                        g[:, (e0 - first) * C:(e1 - first) * C], MULT)
 
-        def scatter(e, n):
-            nc.vector.tensor_tensor(windows[n][:].indirect(slots(e, e + 1)), ysb[e, n], gates[e], MULT)
-
-        def put_back(e, b):
-            routed2(e, 0, NT, b)
-            for n in range(NT):
-                scatter(e, n)
-
-        ys = {}
-
-        def shared2(n, half, b):
+        def finish(n, half, b):
             y = bank(b)
             layer2(y[:], E, n, slice(S + half * BANK, S + (half + 1) * BANK))
-            ys[n, half] = y
-
-        def finish(n, half):
             cols = slice(half * BANK, (half + 1) * BANK)
             res = keep.tile([P, BANK], F32, name="res%d_%d" % (n, half))
-            nc.vector.tensor_tensor(res[:], ys[n, half][:], windows[n][:, cols], ADD)
+            nc.vector.tensor_tensor(res[:], y[:], windows[n][:, cols], ADD)
             nc.sync.dma_start(out[n * P:(n + 1) * P, cols], res[:])
 
-        gather_words(0, E, 0, 1, "gw_first")
-        gather_scales(0, 3, "gs0")
-        gather_words(0, 1, 1, PASSES, "gw0")
-        gather_words(1, 2, 1, PASSES, "gw1")
-        gather_words(2, 4, 1, PASSES, "gw2")
-        gather_words(4, E, 1, PASSES, "gw4")
         warm = bank(7)
         for i in range(WARM):
-            nc.tensor.matmul_mx(out=warm[:], lhsT=xw[0][:, :P].bitcast(FP8X4), lhsT_scale=xs[:, 0, :P],
-                                rhs=w1w[0, 0].bitcast(FP4X4), rhs_scale=xs[:, 0, :H], start=True, stop=True)
-        layer1(0)
-        load_w2(keep, "w1a", 4, E + 1)
-        layer1(1)
-        load_gate(first_late, "w1b", 3, E)
-        turn(0, 1, 3)
-        gather_scales(3, 4, "grouped0")
-        routed2(0, 0, 1, 3)
-        scatter(0, 0)
-        turn(1, 2, 4)
-        gather_scales(4, E, "grouped1")
-        routed2(0, 1, NT, 4)
-        scatter(0, 1)
-        scatter(0, 2)
-        layer1(2)
-        turn(2, 3, 3)
-        put_back(1, 3)
-        layer1(6)
-        layer1(7)
-        turn(6, 8, 5)
-        layer1(3)
-        turn(3, 4, 4)
-        put_back(2, 4)
-        layer1(8)
-        layer1(9)
-        turn(8, 10, 6)
-        layer1(4)
-        turn(4, 5, 3)
-        put_back(3, 3)
-        layer1(10)
-        layer1(11)
-        turn(10, 12, 7)
-        layer1(5)
-        turn(5, 6, 4)
-        put_back(4, 4)
-        layer1(12)
-        layer1(13)
-        routed2(5, 0, NT, 3)
-        turn(12, 14, 5)
-        for n in range(NT):
-            shared2(n, 0, (6, 7, 4)[n])
-            scatter(5, n)
-            finish(n, 0)
-        for n in range(NT):
-            shared2(n, 1, n)
-            finish(n, 1)
+            nc.tensor.matmul_mx(out=warm[:], lhsT=xw[0][:, :P].bitcast(FP8X4), lhsT_scale=xs[:, 1, :P],
+                                rhs=w1w[0][:, 0, :].bitcast(FP4X4), rhs_scale=xs[:, 1, :H], start=True, stop=True)
+        layer1(0, 0)
+        layer1(1, 1)
+        turn_routed(0, 1, 3)
+        put_back(0, 1, 0, 1, 3)
+        turn_routed(1, 2, 4)
+        put_back(0, 1, 1, NT, 4)
+        put_back(1, 2, 0, 2, 3)
+        layer1(2, 2)
+        layer1(3, 0)
+        turn_routed(2, 4, 4)
+        put_back(1, 2, 2, NT, 4)
+        put_back(2, 4, 0, 2, 3)
+        shared = [grouped(E, E + 4), grouped(E + 4, E + 8)]
+        layer1(E, 1)
+        layer1(E + 1, 2)
+        turn(E, E + 2, 5, shared[0][:, :2 * H])
+        layer1(4, 0)
+        layer1(5, 1)
+        turn_routed(4, E, 4)
+        put_back(2, 4, 2, NT, 4)
+        for pair in range(1, 4):
+            i = E + 2 * pair
+            layer1(i, (2 * pair) % 3)
+            layer1(i + 1, (2 * pair + 1) % 3)
+            turn(i, i + 2, 5 + pair % 3, shared[pair // 2][:, (pair % 2) * 2 * H:(pair % 2 + 1) * 2 * H])
+            if pair % 2 == 1:
+                quantise(i - 2, i + 2, shared[pair // 2][:])
+            if pair < 3:
+                put_back(4, E, 2 * pair - 2, min(2 * pair, NT), 5 + pair)
+        for half in range(2):
+            for n in range(NT):
+                finish(n, half, ((3, 4, 6), (7, 2, 5))[half][n])

@@ -24,8 +24,10 @@ NT = N // P
 S = E * C
 BANK = 512
 FIRST = 4
-EARLY = 1
+EARLY = 4
 WARM = 6
+TAIL = 128
+ZW = 16
 LAST = 64
 
 
@@ -60,6 +62,12 @@ def tile_moe_shr_mlp_silu_kernel(tc, x_words, x_scales, w1_words, w1_scales, w2_
         def clear(tile, b0, b1):
             nc.vector.memset(tile[:].rearrange("p a w -> p (a w)")[:, b0:b1].bitcast(I32), 0)
 
+        def fill(tile, b0, b1):
+            words = tile[:].rearrange("p a w -> p (a w)")[:, b0:b1].bitcast(I32)
+            count = (b1 - b0) // (4 * ZW)
+            nc.vector.tensor_copy(words.rearrange("p (c w) -> p c w", w=ZW),
+                                  zeros[:].unsqueeze(1).to_broadcast([P, count, ZW]))
+
         def load_scales(tile, rows):
             for r in range(4):
                 nc.sync.dma_start(tile[r:P:32].bitcast(I32), rows[r:16:4].bitcast(I32))
@@ -87,14 +95,14 @@ def tile_moe_shr_mlp_silu_kernel(tc, x_words, x_scales, w1_words, w1_scales, w2_
         x_planes = x_scales.rearrange("s f t -> f s t")
         w1_planes = w1_scales.rearrange("e s f i -> f (e s) i")
         xs = planes("xs", PASSES, T)
-        w1s_first = planes("w1s_first", FIRST * PASSES, H)
-        w1s_rest = planes("w1s_rest", (E + 1 - FIRST) * PASSES, H)
+        w1s_first = planes("w1s_first", (E + 1 - FIRST) * PASSES, H)
+        w1s_rest = planes("w1s_rest", FIRST * PASSES, H)
         w2s = planes("w2s", E + 1, N)
-        gs_moved = planes("gs_moved", PASSES - 1, S - EARLY * C)
+        gs_moved = planes("gs_moved", PASSES - 1, EARLY * C)
 
         offsets = keep.tile([P, S // 16], U16, name="offsets")
         nc.sync.dma_start(offsets[:], offs)
-        load_w1(keep, 0)
+        load_w1(keep, E)
         xa = keep.tile([P, T], I32, name="xa", align_bytes=64)
         nc.sync.dma_start(xa[:], x_rows[:, 0, :])
         clear(xs, 0, PASSES * T)
@@ -103,65 +111,67 @@ def tile_moe_shr_mlp_silu_kernel(tc, x_words, x_scales, w1_words, w1_scales, w2_
                               x_planes[8 * half:8 * half + 8, 1:, :].bitcast(I32))
         load_scales(xs, x_planes)
 
+        zeros = keep.tile([P, ZW], I32, name="zeros", align_bytes=64)
+        nc.vector.memset(zeros[:], 0)
         late = stage(0)
         xb = late.tile([P, PASSES - 1, T], I32, name="xb", align_bytes=64)
         nc.sync.dma_start(xb[:], x_rows[:, 1:, :])
         xw = [xa[:]] + [xb[:, s, :] for s in range(PASSES - 1)]
         clear_window(0)
-        clear(w1s_first, 0, FIRST * PASSES * H)
-        load_scales(w1s_first, w1_planes[:, :FIRST * PASSES, :])
+        fill(w1s_first, 0, (E + 1 - FIRST) * PASSES * H)
+        load_scales(w1s_first, w1_planes[:, FIRST * PASSES:, :])
+        fill(w2s, LAST, (E + 1) * N)
 
         late = stage(1)
-        load_w1(late, 1)
+        load_w1(late, 5)
+        load_w1(late, 4)
+        load_w2(late, 3, E + 1)
+        load_gate(late, 4, E)
+        clear(w2s, 0, LAST)
+        load_scales(w2s, w2_scales.rearrange("e s f n -> f (e s) n"))
+        load_w1(late, 3)
         ident = late.tile([P, P], F32, name="ident")
         make_identity(nc, ident[:])
         clear_window(1)
-        clear(gs_moved, 0, (PASSES - 1) * (S - EARLY * C))
-        clear(w2s, LAST, (E + 1) * N)
-        clear(w1s_rest, LAST, (E + 1 - FIRST) * PASSES * H)
+        clear(gs_moved, 0, (PASSES - 1) * EARLY * C)
+        fill(w1s_rest, LAST, FIRST * PASSES * H)
 
         gw, gs = {}, {}
 
-        def gather_words(e0, e1, s0, s1):
-            t = keep.tile([P, s1 - s0, (e1 - e0) * C], U32, name="gw%d_%d" % (e0, s0), align_bytes=64)
+        def gather_words(e0, e1, s0, s1, tag=None):
+            t = keep.tile([P, s1 - s0, (e1 - e0) * C], U32, name="gw%d_%d" % (e0, s0), tag=tag or "gw%d_%d" % (e0, s0), align_bytes=64)
             for s in range(s0, s1):
                 nc.vector.tensor_copy(t[:, s - s0, :], xw[s].bitcast(U32).indirect(slots(e0, e1)))
                 for e in range(e0, e1):
                     gw[e, s] = t[:, s - s0, (e - e0) * C:(e - e0 + 1) * C]
 
-        gather_words(0, E, 0, 1)
-        gs_packed = keep.tile([P, S - EARLY * C], U8, name="gs_packed", align_bytes=64)
-        nc.vector.tensor_copy(gs_packed[:], xs[:, 0, :].indirect(slots(EARLY, E)))
+        gather_words(EARLY, E, 0, 1)
+        gs_early = planes("gs_early", PASSES, S - EARLY * C)
+        for s in range(PASSES):
+            nc.vector.tensor_copy(gs_early[:, s, :], xs[:, s, :].indirect(slots(EARLY, E)))
+            for e in range(EARLY, E):
+                gs[e, s] = gs_early[:, s, (e - EARLY) * C:(e - EARLY + 1) * C]
+        gs_packed = keep.tile([P, EARLY * C], U8, name="gs_packed", align_bytes=64)
+        nc.vector.tensor_copy(gs_packed[:], xs[:, 0, :].indirect(slots(0, EARLY)))
         for q in (0, 2, 1, 3):
             first = 64 * (q // 2) + 4 + 8 * (q % 2)
-            nc.scalar.dma_start(gs_moved[32 * q:32 * q + 4].bitcast(I32), gs_packed[first:first + 8].bitcast(I32))
-        for e in range(EARLY, E):
-            cols = slice((e - EARLY) * C, (e - EARLY + 1) * C)
-            gs[e, 0] = gs_packed[:, cols]
+            nc.sync.dma_start(gs_moved[32 * q:32 * q + 4].bitcast(I32), gs_packed[first:first + 8].bitcast(I32))
+        for e in range(EARLY):
+            gs[e, 0] = gs_packed[:, e * C:(e + 1) * C]
             for s in range(1, PASSES):
-                gs[e, s] = gs_moved[:, s - 1, cols]
+                gs[e, s] = gs_moved[:, s - 1, e * C:(e + 1) * C]
 
         late = stage(2)
-        load_w2(late, 0, 4)
-        load_gate(late, 0, 2)
-        clear(w2s, 0, LAST)
-        load_scales(w2s, w2_scales.rearrange("e s f n -> f (e s) n"))
-        load_w1(late, 2)
-        load_w1(late, 3)
-        load_gate(late, 2, E)
         clear(w1s_rest, 0, LAST)
-        load_scales(w1s_rest, w1_planes[:, FIRST * PASSES:, :])
-        for e in (E, 4, 5):
-            load_w1(late, e)
-        load_w2(late, 4, E + 1)
+        load_scales(w1s_rest, w1_planes[:, :FIRST * PASSES, :])
+        load_w1(late, 2)
+        load_w2(late, 0, 3)
+        load_gate(late, 0, 4)
+        load_w1(late, 1)
+        load_w1(late, 0)
         clear_window(2)
-        gs_early = planes("gs_early", PASSES, EARLY * C)
-        for s in range(PASSES):
-            nc.vector.tensor_copy(gs_early[:, s, :], xs[:, s, :].indirect(slots(0, EARLY)))
-            for e in range(EARLY):
-                gs[e, s] = gs_early[:, s, e * C:(e + 1) * C]
-        gather_words(0, 2, 1, PASSES)
-        gather_words(2, E, 1, PASSES)
+        gather_words(EARLY, E, 1, PASSES)
+        gather_words(0, EARLY, 1, PASSES)
 
         hw = keep.tile([P, S + T], U32, name="hw", align_bytes=64)
         hs = keep.tile([P, S + T], U8, name="hs", align_bytes=64)
@@ -177,9 +187,9 @@ def tile_moe_shr_mlp_silu_kernel(tc, x_words, x_scales, w1_words, w1_scales, w2_
                     t0 = (i - E) * P
                     words, scales = xw[s][:, t0:t0 + P], xs[:, s, t0:t0 + P]
                 if e < FIRST:
-                    w_scales = w1s_first[:, e * PASSES + s, :]
+                    w_scales = w1s_rest[:, e * PASSES + s, :]
                 else:
-                    w_scales = w1s_rest[:, (e - FIRST) * PASSES + s, :]
+                    w_scales = w1s_first[:, (e - FIRST) * PASSES + s, :]
                 nc.tensor.matmul_mx(
                     out=a[:], lhsT=words.bitcast(FP8X4), lhsT_scale=scales,
                     rhs=w1w[e][:, s, :].bitcast(FP4X4), rhs_scale=w_scales,
@@ -189,7 +199,7 @@ def tile_moe_shr_mlp_silu_kernel(tc, x_words, x_scales, w1_words, w1_scales, w2_
             hb[i] = h
 
         def grouped(i0, i1):
-            return keep.tile([P, (i1 - i0) * H], BF16, name="grouped%d" % i0, align_bytes=64)
+            return keep.tile([P, (i1 - i0) * H], BF16, name="grouped%d" % i0, tag="grouped%d" % i0, align_bytes=64)
 
         def turn(i0, i1, b, dst):
             k = i1 - i0
@@ -233,45 +243,57 @@ def tile_moe_shr_mlp_silu_kernel(tc, x_words, x_scales, w1_words, w1_scales, w2_
 
         def finish(n, half, b):
             y = bank(b)
-            layer2(y[:], E, n, slice(S + half * BANK, S + (half + 1) * BANK))
-            cols = slice(half * BANK, (half + 1) * BANK)
-            res = keep.tile([P, BANK], F32, name="res%d_%d" % (n, half))
-            nc.vector.tensor_tensor(res[:], y[:], windows[n][:, cols], ADD)
-            nc.sync.dma_start(out[n * P:(n + 1) * P, cols], res[:])
+            t0 = half * BANK
+            layer2(y[:], E, n, slice(S + t0, S + t0 + BANK))
+            cuts = (0, BANK - TAIL, BANK) if (n, half) == (NT - 1, 1) else (0, BANK)
+            for c0, c1 in zip(cuts, cuts[1:]):
+                res = keep.tile([P, c1 - c0], F32, name="res%d_%d" % (n, t0 + c0))
+                nc.vector.tensor_tensor(res[:], y[:, c0:c1], windows[n][:, t0 + c0:t0 + c1], ADD)
+                nc.sync.dma_start(out[n * P:(n + 1) * P, t0 + c0:t0 + c1], res[:])
 
         warm = bank(7)
         for i in range(WARM):
             nc.tensor.matmul_mx(out=warm[:], lhsT=xw[0][:, :P].bitcast(FP8X4), lhsT_scale=xs[:, 1, :P],
-                                rhs=w1w[0][:, 0, :].bitcast(FP4X4), rhs_scale=xs[:, 1, :H], start=True, stop=True)
-        layer1(0, 0)
-        layer1(1, 1)
-        turn_routed(0, 1, 3)
-        put_back(0, 1, 0, 1, 3)
-        turn_routed(1, 2, 4)
-        put_back(0, 1, 1, NT, 4)
-        put_back(1, 2, 0, 2, 3)
-        layer1(2, 2)
-        layer1(3, 0)
-        turn_routed(2, 4, 4)
-        put_back(1, 2, 2, NT, 4)
-        put_back(2, 4, 0, 2, 3)
+                                rhs=w1w[E][:, 0, :].bitcast(FP4X4), rhs_scale=xs[:, 1, :H], start=True, stop=True)
         shared = [grouped(E, E + 4), grouped(E + 4, E + 8)]
-        layer1(E, 1)
-        layer1(E + 1, 2)
-        turn(E, E + 2, 5, shared[0][:, :2 * H])
-        layer1(4, 0)
-        layer1(5, 1)
-        turn_routed(4, E, 4)
-        put_back(2, 4, 2, NT, 4)
-        for pair in range(1, 4):
+
+        def turn_shared(pair, b):
             i = E + 2 * pair
-            layer1(i, (2 * pair) % 3)
-            layer1(i + 1, (2 * pair + 1) % 3)
-            turn(i, i + 2, 5 + pair % 3, shared[pair // 2][:, (pair % 2) * 2 * H:(pair % 2 + 1) * 2 * H])
+            turn(i, i + 2, b, shared[pair // 2][:, (pair % 2) * 2 * H:(pair % 2 + 1) * 2 * H])
             if pair % 2 == 1:
                 quantise(i - 2, i + 2, shared[pair // 2][:])
-            if pair < 3:
-                put_back(4, E, 2 * pair - 2, min(2 * pair, NT), 5 + pair)
+
+        layer1(5, 1)
+        layer1(4, 2)
+        layer1(E, 0)
+        turn_routed(5, 6, 3)
+        gather_words(0, EARLY, 0, 1, "grouped5")
+        put_back(5, 6, 0, 1, 3)
+        turn_routed(4, 5, 4)
+        put_back(5, 6, 1, NT, 4)
+        layer1(E + 1, 0)
+        layer1(E + 2, 1)
+        put_back(4, 5, 0, 2, 1)
+        layer1(E + 3, 2)
+        turn_shared(0, 5)
+        layer1(3, 0)
+        layer1(2, 2)
+        turn_routed(2, 4, 3)
+        put_back(4, 5, 2, NT, 3)
+        put_back(2, 4, 0, 2, 1)
+        turn_shared(1, 6)
+        layer1(1, 0)
+        layer1(0, 2)
+        turn_routed(0, 2, 4)
+        put_back(2, 4, 2, NT, 4)
+        layer1(E + 4, 1)
+        layer1(E + 5, 0)
+        put_back(0, 2, 0, 2, 0)
+        layer1(E + 6, 2)
+        layer1(E + 7, 1)
+        turn_shared(2, 5)
+        turn_shared(3, 6)
+        put_back(0, 2, 2, NT, 6)
         for half in range(2):
             for n in range(NT):
-                finish(n, half, ((3, 4, 6), (7, 2, 5))[half][n])
+                finish(n, half, ((3, 4, 0), (5, 7, 2))[half][n])

@@ -15,6 +15,7 @@ U8 = mybir.dt.uint8
 FP8X4 = mybir.dt.float8_e4m3fn_x4
 FP4X4 = mybir.dt.float4_e2m1fn_x4
 SILU = mybir.ActivationFunctionType.Silu
+COPY = mybir.ActivationFunctionType.Copy
 MULT = mybir.AluOpType.mult
 ADD = mybir.AluOpType.add
 
@@ -23,12 +24,10 @@ PASSES = K // 512
 NT = N // P
 S = E * C
 BANK = 512
+PAIR = 2 * C
 FIRST = 4
-EARLY = 4
-WARM = 6
 TAIL = 128
 ZW = 16
-LAST = 64
 
 
 def tile_moe_shr_mlp_silu_kernel(tc, x_words, x_scales, w1_words, w1_scales, w2_words, w2_scales, gate, offs, out):
@@ -43,11 +42,11 @@ def tile_moe_shr_mlp_silu_kernel(tc, x_words, x_scales, w1_words, w1_scales, w2_
         def slots(e0, e1):
             return offsets[:, e0 * C // 16:e1 * C // 16]
 
-        zero = keep.tile([P, 8 * NT], F32, name="zero")
+        zero = keep.tile([P, 8], F32, name="zero")
         windows = [keep.tile([P, T], F32, name="win%d" % n) for n in range(NT)]
 
-        def clear_window(n):
-            nc.scalar.activation(windows[n][:], zero[:, 8 * n:8 * n + 1].to_broadcast([P, T]), SILU)
+        def clear_window(n, col):
+            nc.scalar.activation(windows[n][:], zero[:, col:col + 1].to_broadcast([P, T]), SILU)
 
         def stage(n):
             with tc.tile_pool(name="setup%d" % n, bufs=1) as setup:
@@ -59,241 +58,252 @@ def tile_moe_shr_mlp_silu_kernel(tc, x_words, x_scales, w1_words, w1_scales, w2_
         def planes(name, count, width):
             return keep.tile([P, count, width], U8, name=name, align_bytes=64)
 
-        def clear(tile, b0, b1):
-            nc.vector.memset(tile[:].rearrange("p a w -> p (a w)")[:, b0:b1].bitcast(I32), 0)
-
-        def fill(tile, b0, b1):
-            words = tile[:].rearrange("p a w -> p (a w)")[:, b0:b1].bitcast(I32)
-            count = (b1 - b0) // (4 * ZW)
+        def fill(tile):
+            words = tile[:].rearrange("p a w -> p (a w)").bitcast(I32)
             nc.vector.tensor_copy(words.rearrange("p (c w) -> p c w", w=ZW),
-                                  zeros[:].unsqueeze(1).to_broadcast([P, count, ZW]))
+                                  zeros[:].unsqueeze(1).to_broadcast([P, words.shape[1] // ZW, ZW]))
 
-        def load_scales(tile, rows):
-            for r in range(4):
+        def load_scales(tile, rows, r0=0, r1=4):
+            for r in range(r0, r1):
                 nc.sync.dma_start(tile[r:P:32].bitcast(I32), rows[r:16:4].bitcast(I32))
 
-        w1w, w2w, gates = {}, {}, {}
+        w1w, w2w, gates, xw = {}, {}, {}, {}
 
-        def load_w1(pool, e):
-            t = pool.tile([P, PASSES, 2 * H], U8, name="w1w%d" % e, align_bytes=64)
-            nc.sync.dma_start(t[:].bitcast(I32), w1_words[e].rearrange("s p b -> p s b").bitcast(I32))
-            w1w[e] = t
+        def load_x(pool, s0, s1):
+            t = pool.tile([P, s1 - s0, T], I32, name="x%d" % s0, align_bytes=64)
+            nc.sync.dma_start(t[:], x_rows[:, s0:s1, :])
+            for s in range(s0, s1):
+                xw[s] = t[:, s - s0, :]
+
+        def load_w1(pool, e0, e1):
+            t = pool.tile([P, (e1 - e0) * PASSES, 2 * H], U8, name="w1w%d" % e0, align_bytes=64)
+            nc.sync.dma_start(t[:].bitcast(I32), w1_rows[:, e0 * PASSES:e1 * PASSES, :])
+            for e in range(e0, e1):
+                w1w[e] = t[:, (e - e0) * PASSES:(e - e0 + 1) * PASSES, :]
 
         def load_w2(pool, e0, e1):
             t = pool.tile([P, e1 - e0, 2 * N], U8, name="w2w%d" % e0, align_bytes=64)
-            nc.sync.dma_start(t[:].bitcast(I32), w2_words[e0:e1].rearrange("e s p b -> p (e s) b").bitcast(I32))
+            nc.sync.dma_start(t[:].bitcast(I32), w2_rows[:, e0:e1, :])
             for e in range(e0, e1):
                 w2w[e] = t[:, e - e0, :]
 
         def load_gate(pool, e0, e1):
-            g = pool.tile([P, (e1 - e0) * C], F32, name="gate%d" % e0)
+            g = pool.tile([P, (e1 - e0) * C], F32, name="gate%d" % e0, tag="gate%d" % e0, align_bytes=64)
             nc.sync.dma_start(g[:], gate[:P, e0 * C:e1 * C])
             for e in range(e0, e1):
                 gates[e] = (g, e0)
 
         x_rows = x_words.rearrange("s p t r -> p s (t r)").bitcast(I32)
-        x_planes = x_scales.rearrange("s f t -> f s t")
+        w1_rows = w1_words.rearrange("e s p b -> p (e s) b").bitcast(I32)
+        w2_rows = w2_words.rearrange("e s p b -> p (e s) b").bitcast(I32)
         w1_planes = w1_scales.rearrange("e s f i -> f (e s) i")
         xs = planes("xs", PASSES, T)
-        w1s_first = planes("w1s_first", (E + 1 - FIRST) * PASSES, H)
-        w1s_rest = planes("w1s_rest", FIRST * PASSES, H)
         w2s = planes("w2s", E + 1, N)
-        gs_moved = planes("gs_moved", PASSES - 1, EARLY * C)
+        sets = ((E, E + 1), (FIRST, E), (0, FIRST))
+        w1s = {e0: planes("w1s%d" % e0, (e1 - e0) * PASSES, H) for e0, e1 in sets}
 
+        def load_w1_scales(e0, e1):
+            load_scales(w1s[e0], w1_planes[:, e0 * PASSES:e1 * PASSES, :])
+
+        ident = keep.tile([P, P], F32, name="ident")
+        make_identity(nc, ident[:])
         offsets = keep.tile([P, S // 16], U16, name="offsets")
         nc.sync.dma_start(offsets[:], offs)
-        load_w1(keep, E)
-        xa = keep.tile([P, T], I32, name="xa", align_bytes=64)
-        nc.sync.dma_start(xa[:], x_rows[:, 0, :])
-        clear(xs, 0, PASSES * T)
-        for half in range(2):
-            nc.sync.dma_start(xs[64 * half + 4:64 * half + 20, 0, :].bitcast(I32),
-                              x_planes[8 * half:8 * half + 8, 1:, :].bitcast(I32))
-        load_scales(xs, x_planes)
-
+        load_x(keep, 0, 1)
+        load_w1(keep, E, E + 1)
+        nc.vector.memset(xs[:].rearrange("p a w -> p (a w)").bitcast(I32), 0)
+        load_scales(xs, x_scales.rearrange("s f t -> f s t"))
         zeros = keep.tile([P, ZW], I32, name="zeros", align_bytes=64)
         nc.vector.memset(zeros[:], 0)
-        late = stage(0)
-        xb = late.tile([P, PASSES - 1, T], I32, name="xb", align_bytes=64)
-        nc.sync.dma_start(xb[:], x_rows[:, 1:, :])
-        xw = [xa[:]] + [xb[:, s, :] for s in range(PASSES - 1)]
-        clear_window(0)
-        fill(w1s_first, 0, (E + 1 - FIRST) * PASSES * H)
-        load_scales(w1s_first, w1_planes[:, FIRST * PASSES:, :])
-        fill(w2s, LAST, (E + 1) * N)
+        fill(w1s[E])
+        load_w1_scales(E, E + 1)
+        fill(w1s[FIRST])
+        fill(w2s)
+        fill(w1s[0])
 
-        late = stage(1)
-        load_w1(late, 5)
-        load_w1(late, 4)
-        load_w2(late, 3, E + 1)
+        late = stage(0)
+        for n in range(NT):
+            clear_window(n, 0)
+        load_x(late, 1, PASSES)
+        load_w1(late, 5, 6)
+        load_w1_scales(FIRST, E)
+        load_w1(late, 4, 5)
+        load_w2(late, 4, E + 1)
         load_gate(late, 4, E)
-        clear(w2s, 0, LAST)
         load_scales(w2s, w2_scales.rearrange("e s f n -> f (e s) n"))
-        load_w1(late, 3)
-        ident = late.tile([P, P], F32, name="ident")
-        make_identity(nc, ident[:])
-        clear_window(1)
-        clear(gs_moved, 0, (PASSES - 1) * EARLY * C)
-        fill(w1s_rest, LAST, FIRST * PASSES * H)
+        load_w1(late, 2, 4)
+        load_w1_scales(0, FIRST)
+        load_w1(late, 1, 2)
+        load_w1(late, 0, 1)
+        load_w2(late, 0, 4)
+        load_gate(late, 0, 4)
 
         gw, gs = {}, {}
 
-        def gather_words(e0, e1, s0, s1, tag=None):
-            t = keep.tile([P, s1 - s0, (e1 - e0) * C], U32, name="gw%d_%d" % (e0, s0), tag=tag or "gw%d_%d" % (e0, s0), align_bytes=64)
+        def gather_words(e0, e1, s, tag=None):
+            name = "gw%d_%d" % (e0, s)
+            t = late.tile([P, (e1 - e0) * C], U32, name=name, tag=tag or name, align_bytes=64)
+            nc.vector.tensor_copy(t[:], xw[s].bitcast(U32).indirect(slots(e0, e1)))
+            for e in range(e0, e1):
+                gw[e, s] = t[:, (e - e0) * C:(e - e0 + 1) * C]
+
+        def gather_scales(e0, e1, s0, s1, tag=None):
+            name = "gs%d_%d" % (e0, s0)
+            t = late.tile([P, s1 - s0, (e1 - e0) * C], U8, name=name, tag=tag or name, align_bytes=64)
             for s in range(s0, s1):
-                nc.vector.tensor_copy(t[:, s - s0, :], xw[s].bitcast(U32).indirect(slots(e0, e1)))
+                nc.vector.tensor_copy(t[:, s - s0, :], xs[:, s, :].indirect(slots(e0, e1)))
                 for e in range(e0, e1):
-                    gw[e, s] = t[:, s - s0, (e - e0) * C:(e - e0 + 1) * C]
+                    gs[e, s] = t[:, s - s0, (e - e0) * C:(e - e0 + 1) * C]
+            return t
 
-        gather_words(EARLY, E, 0, 1)
-        gs_early = planes("gs_early", PASSES, S - EARLY * C)
-        for s in range(PASSES):
-            nc.vector.tensor_copy(gs_early[:, s, :], xs[:, s, :].indirect(slots(EARLY, E)))
-            for e in range(EARLY, E):
-                gs[e, s] = gs_early[:, s, (e - EARLY) * C:(e - EARLY + 1) * C]
-        gs_packed = keep.tile([P, EARLY * C], U8, name="gs_packed", align_bytes=64)
-        nc.vector.tensor_copy(gs_packed[:], xs[:, 0, :].indirect(slots(0, EARLY)))
-        for q in (0, 2, 1, 3):
-            first = 64 * (q // 2) + 4 + 8 * (q % 2)
-            nc.sync.dma_start(gs_moved[32 * q:32 * q + 4].bitcast(I32), gs_packed[first:first + 8].bitcast(I32))
-        for e in range(EARLY):
-            gs[e, 0] = gs_packed[:, e * C:(e + 1) * C]
-            for s in range(1, PASSES):
-                gs[e, s] = gs_moved[:, s - 1, e * C:(e + 1) * C]
+        hb, codes = {}, {}
 
-        late = stage(2)
-        clear(w1s_rest, 0, LAST)
-        load_scales(w1s_rest, w1_planes[:, :FIRST * PASSES, :])
-        load_w1(late, 2)
-        load_w2(late, 0, 3)
-        load_gate(late, 0, 4)
-        load_w1(late, 1)
-        load_w1(late, 0)
-        clear_window(2)
-        gather_words(EARLY, E, 1, PASSES)
-        gather_words(0, EARLY, 1, PASSES)
-
-        hw = keep.tile([P, S + T], U32, name="hw", align_bytes=64)
-        hs = keep.tile([P, S + T], U8, name="hs", align_bytes=64)
-        hb, ysb, ys = {}, {}, {}
-
-        def layer1(i, b):
-            a = bank(b)
+        def first_pass(a, i, s):
             e = min(i, E)
-            for s in range(PASSES):
-                if i < E:
-                    words, scales = gw[i, s], gs[i, s]
-                else:
-                    t0 = (i - E) * P
-                    words, scales = xw[s][:, t0:t0 + P], xs[:, s, t0:t0 + P]
-                if e < FIRST:
-                    w_scales = w1s_rest[:, e * PASSES + s, :]
-                else:
-                    w_scales = w1s_first[:, (e - FIRST) * PASSES + s, :]
-                nc.tensor.matmul_mx(
-                    out=a[:], lhsT=words.bitcast(FP8X4), lhsT_scale=scales,
-                    rhs=w1w[e][:, s, :].bitcast(FP4X4), rhs_scale=w_scales,
-                    start=(s == 0), stop=(s == PASSES - 1))
+            if i < E:
+                words, scales = gw[i, s], gs[i, s]
+            else:
+                t0 = (i - E) * P
+                words, scales = xw[s][:, t0:t0 + P], xs[:, s, t0:t0 + P]
+            e0 = max(first for first, last in sets if first <= e)
+            w_scales = w1s[e0][:, (e - e0) * PASSES + s, :]
+            nc.tensor.matmul_mx(
+                out=a[:], lhsT=words.bitcast(FP8X4), lhsT_scale=scales,
+                rhs=w1w[e][:, s, :].bitcast(FP4X4), rhs_scale=w_scales,
+                start=(s == 0), stop=(s == PASSES - 1))
+
+        def activate(a, i):
             h = keep.tile([P, 2, P, 2], BF16, name="h%d" % i)
             nc.scalar.activation(h[:], a[:].rearrange("t (p u e) -> t u p e", u=2, e=2), SILU)
             hb[i] = h
 
-        def grouped(i0, i1):
-            return keep.tile([P, (i1 - i0) * H], BF16, name="grouped%d" % i0, tag="grouped%d" % i0, align_bytes=64)
+        def layer1(i, b, opened=None):
+            a = bank(b) if opened is None else opened
+            for s in range(0 if opened is None else 1, PASSES):
+                first_pass(a, i, s)
+            activate(a, i)
 
-        def turn(i0, i1, b, dst):
-            k = i1 - i0
-            tr = bank(b)[:].rearrange("p (h w t) -> p h w t", h=2, w=2)
+        def grouped(i0, i1):
+            return late.tile([P, (i1 - i0) * H], BF16, name="grouped%d" % i0, tag="grouped%d" % i0, align_bytes=64)
+
+        def turn(i0, i1, b, dst, copy):
+            tr = bank(b)[:].rearrange("p (h w t) -> p h w t", h=2, w=2)[:, :i1 - i0]
             for i in range(i0, i1):
                 words = hb[i][:].rearrange("t u p e -> t (u p e)").bitcast(F32)
                 for w in range(2):
                     nc.tensor.transpose(tr[:, i - i0, w, :], words[:, w * P:(w + 1) * P], ident[:])
-            nc.scalar.copy(dst.bitcast(F32).rearrange("p (h t w) -> p h t w", h=k, w=2),
-                           tr[:, :k, :, :].rearrange("p h w t -> p h t w"))
+            copy(dst.bitcast(F32).rearrange("p (h t w) -> p h t w", h=i1 - i0, w=2), tr.rearrange("p h w t -> p h t w"))
 
-        def quantise(i0, i1, src):
-            cols = slice(i0 * P, i1 * P)
-            nc.vector.quantize_mx(out=hw[:, cols].bitcast(FP8X4), scales=hs[:, cols], in_=src)
+        def quantise(i0, i1, src, tag=None):
+            hw = late.tile([P, (i1 - i0) * P], U32, name="hw%d" % i0, tag=tag or "hw%d" % i0, align_bytes=64)
+            hs = late.tile([P, (i1 - i0) * P], U8, name="hs%d" % i0, align_bytes=64)
+            nc.vector.quantize_mx(out=hw[:].bitcast(FP8X4), scales=hs[:], in_=src)
+            for i in range(i0, i1):
+                codes[i] = (hw, hs, i0)
 
-        def turn_routed(e0, e1, b):
+        def turn_routed(e0, e1, b, copy):
             g = grouped(e0, e1)
-            turn(e0, e1, b, g[:])
+            turn(e0, e1, b, g[:], copy)
             quantise(e0, e1, g[:])
 
-        def layer2(dst, e, n, cols):
+        def layer2(dst, e, n, i0, i1):
+            hw, hs, first = codes[i0]
+            cols = slice((i0 - first) * P, (i1 - first) * P)
             nc.tensor.matmul_mx(
                 out=dst, lhsT=w2w[e][:, n * 2 * P:(n + 1) * 2 * P].bitcast(FP4X4),
                 lhsT_scale=w2s[:, e, n * P:(n + 1) * P],
                 rhs=hw[:, cols].bitcast(FP8X4), rhs_scale=hs[:, cols], start=True, stop=True)
 
-        def put_back(e0, e1, n0, n1, b):
-            y = bank(b)
-            width = (e1 - e0) * C
-            for n in range(n0, n1):
-                for e in range(e0, e1):
-                    c0 = (n - n0) * width + (e - e0) * C
-                    layer2(y[:, c0:c0 + C], e, n, slice(e * C, (e + 1) * C))
-            t = keep.tile([P, (n1 - n0) * width], F32, name="y%d_%d" % (e0, n0))
-            nc.scalar.copy(t[:], y[:, :(n1 - n0) * width])
-            g, first = gates[e0]
-            for n in range(n0, n1):
-                ysb[e0, n] = t[:, (n - n0) * width:(n - n0 + 1) * width]
-                nc.vector.tensor_tensor(windows[n][:].indirect(slots(e0, e1)), ysb[e0, n],
-                                        g[:, (e0 - first) * C:(e1 - first) * C], MULT)
+        ys = {}
 
-        def finish(n, half, b):
+        gated = late.tile([P, NT, S], F32, name="gated", align_bytes=64)
+
+        def second(e0, e1, n0, n1, b, step=1):
+            blocks = range(n0, n1, step)
+            y = bank(b)[:, :len(blocks) * (e1 - e0) * C].rearrange("p (n c) -> p n c", n=len(blocks))
+            for k, n in enumerate(blocks):
+                for e in range(e0, e1):
+                    layer2(y[:, k, (e - e0) * C:(e - e0 + 1) * C], e, n, e, e + 1)
+            g, first = gates[e0]
+            weights = g[:, (e0 - first) * C:(e1 - first) * C].unsqueeze(1).to_broadcast([P, len(blocks), (e1 - e0) * C])
+            nc.vector.tensor_tensor(gated[:, n0:n1:step, e0 * C:e1 * C], y, weights, MULT)
+
+        def scatter(e0, e1, n, copy):
+            copy(windows[n][:].indirect(slots(e0, e1)), gated[:, n, e0 * C:e1 * C])
+
+        def by_scalar(dst, src):
+            nc.scalar.activation(dst, src, COPY)
+
+        def finish(n, half, b, cuts):
             y = bank(b)
             t0 = half * BANK
-            layer2(y[:], E, n, slice(S + t0, S + t0 + BANK))
-            cuts = (0, BANK - TAIL, BANK) if (n, half) == (NT - 1, 1) else (0, BANK)
+            layer2(y[:], E, n, E + 4 * half, E + 4 * half + 4)
             for c0, c1 in zip(cuts, cuts[1:]):
                 res = keep.tile([P, c1 - c0], F32, name="res%d_%d" % (n, t0 + c0))
                 nc.vector.tensor_tensor(res[:], y[:, c0:c1], windows[n][:, t0 + c0:t0 + c1], ADD)
                 nc.sync.dma_start(out[n * P:(n + 1) * P, t0 + c0:t0 + c1], res[:])
 
-        warm = bank(7)
-        for i in range(WARM):
-            nc.tensor.matmul_mx(out=warm[:], lhsT=xw[0][:, :P].bitcast(FP8X4), lhsT_scale=xs[:, 1, :P],
-                                rhs=w1w[E][:, 0, :].bitcast(FP4X4), rhs_scale=xs[:, 1, :H], start=True, stop=True)
         shared = [grouped(E, E + 4), grouped(E + 4, E + 8)]
 
-        def turn_shared(pair, b):
+        def turn_shared(pair, b, copy, tag=None):
             i = E + 2 * pair
-            turn(i, i + 2, b, shared[pair // 2][:, (pair % 2) * 2 * H:(pair % 2 + 1) * 2 * H])
+            turn(i, i + 2, b, shared[pair // 2][:, (pair % 2) * 2 * H:(pair % 2 + 1) * 2 * H], copy)
             if pair % 2 == 1:
-                quantise(i - 2, i + 2, shared[pair // 2][:])
+                quantise(i - 2, i + 2, shared[pair // 2][:], tag)
 
-        layer1(5, 1)
-        layer1(4, 2)
-        layer1(E, 0)
-        turn_routed(5, 6, 3)
-        gather_words(0, EARLY, 0, 1, "grouped5")
-        put_back(5, 6, 0, 1, 3)
-        turn_routed(4, 5, 4)
-        put_back(5, 6, 1, NT, 4)
-        layer1(E + 1, 0)
-        layer1(E + 2, 1)
-        put_back(4, 5, 0, 2, 1)
-        layer1(E + 3, 2)
-        turn_shared(0, 5)
-        layer1(3, 0)
-        layer1(2, 2)
-        turn_routed(2, 4, 3)
-        put_back(4, 5, 2, NT, 3)
-        put_back(2, 4, 0, 2, 1)
-        turn_shared(1, 6)
-        layer1(1, 0)
-        layer1(0, 2)
-        turn_routed(0, 2, 4)
-        put_back(2, 4, 2, NT, 4)
-        layer1(E + 4, 1)
-        layer1(E + 5, 0)
-        put_back(0, 2, 0, 2, 0)
-        layer1(E + 6, 2)
-        layer1(E + 7, 1)
-        turn_shared(2, 5)
-        turn_shared(3, 6)
-        put_back(0, 2, 2, NT, 6)
-        for half in range(2):
-            for n in range(NT):
-                finish(n, half, ((3, 4, 0), (5, 7, 2))[half][n])
+        on_scalar, on_vector = nc.scalar.copy, nc.vector.tensor_copy
+
+        gather_words(0, E, 0)
+        gather_scales(2, E, 0, PASSES)
+        for s in range(1, PASSES):
+            gather_words(4, E, s)
+        for s in range(1, PASSES):
+            gather_words(0, 4, s)
+
+        opened = [bank(b) for b in range(3)]
+        for b in range(3):
+            first_pass(opened[b], E + b, 0)
+        for b in range(3):
+            layer1(E + b, b, opened[b])
+        layer1(5, 4)
+        layer1(4, 5)
+        gather_scales(0, 2, 0, PASSES, "gw4_2")
+        layer1(E + 3, 4)
+        turn_routed(4, E, 5, on_scalar)
+        layer1(E + 4, 4)
+        second(4, E, 0, 1, 0)
+        scatter(4, E, 0, by_scalar)
+        second(4, E, 1, NT, 1)
+        scatter(4, E, 1, on_vector)
+        scatter(4, E, 2, on_vector)
+        layer1(3, 2)
+        layer1(2, 3)
+        layer1(1, 6)
+        layer1(0, 7)
+        turn_routed(2, 4, 5, on_vector)
+        turn(E, E + 2, 2, shared[0][:, :2 * H], on_scalar)
+        turn_routed(0, 2, 0, on_vector)
+        turn(E + 2, E + 4, 3, shared[0][:, 2 * H:], on_scalar)
+        layer1(E + 5, 6)
+        second(2, 4, 0, NT, 4, 2)
+        scatter(2, 4, 0, by_scalar)
+        quantise(E, E + 4, shared[0][:])
+        scatter(2, 4, 2, on_vector)
+        layer1(E + 6, 7)
+        layer1(E + 7, 5)
+        turn_shared(2, 2, on_scalar)
+        second(0, 2, 0, NT, 1, 2)
+        scatter(0, 2, 0, by_scalar)
+        second(0, 4, 1, 2, 0)
+        scatter(2, 4, 1, by_scalar)
+        scatter(0, 2, 1, by_scalar)
+        scatter(0, 2, 2, on_vector)
+        turn(E + 6, E + 8, 3, shared[1][:, 2 * H:], on_vector)
+        quantise(E + 4, E + 8, shared[1][:])
+        whole = (0, BANK)
+        finish(2, 0, 0, whole)
+        finish(0, 0, 3, whole)
+        finish(2, 1, 6, whole)
+        finish(0, 1, 4, whole)
+        finish(1, 0, 0, whole)
+        finish(1, 1, 7, (0, BANK - TAIL, BANK))

@@ -99,7 +99,7 @@ def tile_moe_shr_mlp_silu_kernel(tc, x_words, x_scales, w1_words, w1_scales, w2_
         w1_planes = w1_scales.rearrange("e s f i -> f (e s) i")
         xs = planes("xs", PASSES, T)
         w2s = planes("w2s", E + 1, N)
-        sets = ((E, E + 1), (FIRST, E), (0, FIRST))
+        sets = ((E, E + 1), (4, E), (0, 4))
         w1s = {e0: planes("w1s%d" % e0, (e1 - e0) * PASSES, H) for e0, e1 in sets}
 
         def load_w1_scales(e0, e1):
@@ -117,7 +117,7 @@ def tile_moe_shr_mlp_silu_kernel(tc, x_words, x_scales, w1_words, w1_scales, w2_
         nc.vector.memset(zeros[:], 0)
         fill(w1s[E])
         load_w1_scales(E, E + 1)
-        fill(w1s[FIRST])
+        fill(w1s[4])
         fill(w2s)
         fill(w1s[0])
 
@@ -125,16 +125,14 @@ def tile_moe_shr_mlp_silu_kernel(tc, x_words, x_scales, w1_words, w1_scales, w2_
         for n in range(NT):
             clear_window(n, 0)
         load_x(late, 1, PASSES)
-        load_w1(late, 5, 6)
-        load_w1_scales(FIRST, E)
-        load_w1(late, 4, 5)
+        load_w1(late, 4, E)
+        load_scales(w2s, w2_scales.rearrange("e s f n -> f (e s) n"))
+        load_w1_scales(4, E)
         load_w2(late, 4, E + 1)
         load_gate(late, 4, E)
-        load_scales(w2s, w2_scales.rearrange("e s f n -> f (e s) n"))
         load_w1(late, 2, 4)
-        load_w1_scales(0, FIRST)
-        load_w1(late, 1, 2)
-        load_w1(late, 0, 1)
+        load_w1_scales(0, 4)
+        load_w1(late, 0, 2)
         load_w2(late, 0, 4)
         load_gate(late, 0, 4)
 
@@ -260,50 +258,50 @@ def tile_moe_shr_mlp_silu_kernel(tc, x_words, x_scales, w1_words, w1_scales, w2_
         for s in range(1, PASSES):
             gather_words(0, 4, s)
 
-        opened = [bank(b) for b in range(3)]
-        for b in range(3):
+        opened = [bank(b) for b in range(4)]
+        for b in range(4):
             first_pass(opened[b], E + b, 0)
-        for b in range(3):
+        for b in range(4):
             layer1(E + b, b, opened[b])
+        layer1(E + 4, 0)
+        layer1(E + 5, 1)
         layer1(5, 4)
         layer1(4, 5)
         gather_scales(0, 2, 0, PASSES, "gw4_2")
-        layer1(E + 3, 4)
+        turn(E, E + 2, 4, shared[0][:, :2 * H], on_scalar)
         turn_routed(4, E, 5, on_scalar)
-        layer1(E + 4, 4)
-        second(4, E, 0, 1, 0)
+        turn(E + 2, E + 4, 4, shared[0][:, 2 * H:], on_scalar)
+        quantise(E, E + 4, shared[0][:])
+        layer1(E + 6, 5)
+        second(4, E, 0, 1, 2)
         scatter(4, E, 0, by_scalar)
-        second(4, E, 1, NT, 1)
+        second(4, E, 1, NT, 3)
         scatter(4, E, 1, on_vector)
         scatter(4, E, 2, on_vector)
-        layer1(3, 2)
-        layer1(2, 3)
-        layer1(1, 6)
-        layer1(0, 7)
-        turn_routed(2, 4, 5, on_vector)
-        turn(E, E + 2, 2, shared[0][:, :2 * H], on_scalar)
-        turn_routed(0, 2, 0, on_vector)
-        turn(E + 2, E + 4, 3, shared[0][:, 2 * H:], on_scalar)
-        layer1(E + 5, 6)
-        second(2, 4, 0, NT, 4, 2)
+        layer1(E + 7, 4)
+        turn(E + 4, E + 6, 2, shared[1][:, :2 * H], on_vector)
+        layer1(3, 0)
+        layer1(2, 6)
+        layer1(1, 1)
+        turn_routed(2, 4, 7, on_vector)
+        layer1(0, 5)
+        turn(E + 6, E + 8, 6, shared[1][:, 2 * H:], on_scalar)
+        second(2, 4, 0, NT, 3, 2)
+        turn_routed(0, 2, 1, on_scalar)
         scatter(2, 4, 0, by_scalar)
-        quantise(E, E + 4, shared[0][:])
-        scatter(2, 4, 2, on_vector)
-        layer1(E + 6, 7)
-        layer1(E + 7, 5)
-        turn_shared(2, 2, on_scalar)
-        second(0, 2, 0, NT, 1, 2)
-        scatter(0, 2, 0, by_scalar)
-        second(0, 4, 1, 2, 0)
+        second(2, 4, 1, 2, 0)
         scatter(2, 4, 1, by_scalar)
+        scatter(2, 4, 2, on_vector)
+        second(0, 2, 0, 2, 2)
+        scatter(0, 2, 0, by_scalar)
         scatter(0, 2, 1, by_scalar)
-        scatter(0, 2, 2, on_vector)
-        turn(E + 6, E + 8, 3, shared[1][:, 2 * H:], on_vector)
+        second(0, 2, 2, 3, 7)
         quantise(E + 4, E + 8, shared[1][:])
+        scatter(0, 2, 2, on_vector)
         whole = (0, BANK)
-        finish(2, 0, 0, whole)
-        finish(0, 0, 3, whole)
-        finish(2, 1, 6, whole)
-        finish(0, 1, 4, whole)
-        finish(1, 0, 0, whole)
-        finish(1, 1, 7, (0, BANK - TAIL, BANK))
+        finish(2, 0, 1, whole)
+        finish(2, 1, 5, whole)
+        finish(0, 0, 7, whole)
+        finish(0, 1, 2, whole)
+        finish(1, 0, 1, whole)
+        finish(1, 1, 5, (0, BANK - TAIL, BANK))

@@ -129,12 +129,12 @@ def tile_moe_shr_mlp_silu_kernel(tc, x_words, x_scales, w1_words, w1_scales, w2_
         load_scales(w2s, w2_scales.rearrange("e s f n -> f (e s) n"))
         load_w1_scales(4, E)
         load_w2(late, 4, E + 1)
-        load_gate(late, 4, E)
+        load_gate(late, 0, E)
         load_w1(late, 2, 4)
         load_w1_scales(0, 4)
-        load_w1(late, 0, 2)
+        load_w1(late, 1, 2)
+        load_w1(late, 0, 1)
         load_w2(late, 0, 4)
-        load_gate(late, 0, 4)
 
         gw, gs = {}, {}
 
@@ -270,21 +270,21 @@ def tile_moe_shr_mlp_silu_kernel(tc, x_words, x_scales, w1_words, w1_scales, w2_
         gather_scales(0, 2, 0, PASSES, "gw4_2")
         turn(E, E + 2, 4, shared[0][:, :2 * H], on_scalar)
         turn_routed(4, E, 5, on_scalar)
-        turn(E + 2, E + 4, 4, shared[0][:, 2 * H:], on_scalar)
-        quantise(E, E + 4, shared[0][:])
-        layer1(E + 6, 5)
+        layer1(E + 6, 4)
+        turn(E + 2, E + 4, 5, shared[0][:, 2 * H:], on_scalar)
         second(4, E, 0, 1, 2)
         scatter(4, E, 0, by_scalar)
         second(4, E, 1, NT, 3)
         scatter(4, E, 1, on_vector)
         scatter(4, E, 2, on_vector)
+        quantise(E, E + 4, shared[0][:])
         layer1(E + 7, 4)
-        turn(E + 4, E + 6, 2, shared[1][:, :2 * H], on_vector)
         layer1(3, 0)
         layer1(2, 6)
         layer1(1, 1)
         turn_routed(2, 4, 7, on_vector)
         layer1(0, 5)
+        turn(E + 4, E + 6, 0, shared[1][:, :2 * H], on_scalar)
         turn(E + 6, E + 8, 6, shared[1][:, 2 * H:], on_scalar)
         second(2, 4, 0, NT, 3, 2)
         turn_routed(0, 2, 1, on_scalar)

@@ -24,8 +24,7 @@ PASSES = K // 512
 NT = N // P
 S = E * C
 BANK = 512
-PAIR = 2 * C
-FIRST = 4
+LEAD = 256
 TAIL = 128
 ZW = 16
 
@@ -36,155 +35,140 @@ def tile_moe_shr_mlp_silu_kernel(tc, x_words, x_scales, w1_words, w1_scales, w2_
         keep = ctx.enter_context(tc.tile_pool(name="keep", bufs=1))
         psum = ctx.enter_context(tc.psum_pool(name="psum", bufs=1))
 
+        banks = [psum.tile([P, BANK], F32, name="bank%d" % b) for b in range(8)]
+
         def bank(b):
-            return psum.tile([P, BANK], F32, name="bank%d" % b, tag="bank%d" % b)
+            return banks[b]
+
+        def sbuf(name, shape, dtype):
+            return keep.tile(shape, dtype, name=name, align_bytes=64)
 
         def slots(e0, e1):
             return offsets[:, e0 * C // 16:e1 * C // 16]
-
-        zero = keep.tile([P, 8], F32, name="zero")
-        windows = [keep.tile([P, T], F32, name="win%d" % n) for n in range(NT)]
-
-        def clear_window(n, col):
-            nc.scalar.activation(windows[n][:], zero[:, col:col + 1].to_broadcast([P, T]), SILU)
-
-        def stage(n):
-            with tc.tile_pool(name="setup%d" % n, bufs=1) as setup:
-                staged = setup.tile([P, 1], F32, name="staged")
-                nc.vector.memset(staged[:], 0.0)
-                nc.vector.tensor_copy(zero[:, 8 * n:8 * n + 1], staged[:])
-            return ctx.enter_context(tc.tile_pool(name="late%d" % n, bufs=1))
-
-        def planes(name, count, width):
-            return keep.tile([P, count, width], U8, name=name, align_bytes=64)
-
-        def fill(tile):
-            words = tile[:].rearrange("p a w -> p (a w)").bitcast(I32)
-            nc.vector.tensor_copy(words.rearrange("p (c w) -> p c w", w=ZW),
-                                  zeros[:].unsqueeze(1).to_broadcast([P, words.shape[1] // ZW, ZW]))
-
-        def load_scales(tile, rows, r0=0, r1=4):
-            for r in range(r0, r1):
-                nc.sync.dma_start(tile[r:P:32].bitcast(I32), rows[r:16:4].bitcast(I32))
-
-        w1w, w2w, gates, xw = {}, {}, {}, {}
-
-        def load_x(pool, s0, s1):
-            t = pool.tile([P, s1 - s0, T], I32, name="x%d" % s0, align_bytes=64)
-            nc.sync.dma_start(t[:], x_rows[:, s0:s1, :])
-            for s in range(s0, s1):
-                xw[s] = t[:, s - s0, :]
-
-        def load_w1(pool, e0, e1):
-            t = pool.tile([P, (e1 - e0) * PASSES, 2 * H], U8, name="w1w%d" % e0, align_bytes=64)
-            nc.sync.dma_start(t[:].bitcast(I32), w1_rows[:, e0 * PASSES:e1 * PASSES, :])
-            for e in range(e0, e1):
-                w1w[e] = t[:, (e - e0) * PASSES:(e - e0 + 1) * PASSES, :]
-
-        def load_w2(pool, e0, e1):
-            t = pool.tile([P, e1 - e0, 2 * N], U8, name="w2w%d" % e0, align_bytes=64)
-            nc.sync.dma_start(t[:].bitcast(I32), w2_rows[:, e0:e1, :])
-            for e in range(e0, e1):
-                w2w[e] = t[:, e - e0, :]
-
-        def load_gate(pool, e0, e1):
-            g = pool.tile([P, (e1 - e0) * C], F32, name="gate%d" % e0, tag="gate%d" % e0, align_bytes=64)
-            nc.sync.dma_start(g[:], gate[:P, e0 * C:e1 * C])
-            for e in range(e0, e1):
-                gates[e] = (g, e0)
 
         x_rows = x_words.rearrange("s p t r -> p s (t r)").bitcast(I32)
         w1_rows = w1_words.rearrange("e s p b -> p (e s) b").bitcast(I32)
         w2_rows = w2_words.rearrange("e s p b -> p (e s) b").bitcast(I32)
         w1_planes = w1_scales.rearrange("e s f i -> f (e s) i")
-        xs = planes("xs", PASSES, T)
-        w2s = planes("w2s", E + 1, N)
-        sets = ((E, E + 1), (4, E), (0, 4))
-        w1s = {e0: planes("w1s%d" % e0, (e1 - e0) * PASSES, H) for e0, e1 in sets}
+
+        offsets = keep.tile([P, S // 16], U16, name="offsets")
+        xw = sbuf("xw", [P, PASSES, T], I32)
+        xs = sbuf("xs", [P, PASSES, T], U8)
+        w2s = sbuf("w2s", [P, E + 1, N], U8)
+        sets = ((E, E + 1), (0, E))
+        w1s = {e0: sbuf("w1s%d" % e0, [P, (e1 - e0) * PASSES, H], U8) for e0, e1 in sets}
+        zeros = sbuf("zeros", [P, ZW], I32)
+        ident = sbuf("ident", [P, P], F32)
+        windows = [sbuf("win%d" % n, [P, T], F32) for n in range(NT)]
+
+        nc.gpsimd.memset(w1s[E][:].rearrange("p a w -> p (a w)").bitcast(I32), 0)
+        nc.vector.memset(xs[:].rearrange("p a w -> p (a w)").bitcast(I32), 0)
+        nc.vector.memset(zeros[:], 0)
+        for tile in (w1s[0], w2s):
+            words = tile[:].rearrange("p a w -> p (a w)").bitcast(I32)
+            nc.vector.tensor_copy(words.rearrange("p (c w) -> p c w", w=ZW),
+                                  zeros[:].unsqueeze(1).to_broadcast([P, words.shape[1] // ZW, ZW]))
+        make_identity(nc, ident[:])
+        nc.gpsimd.memset(windows[2][:], 0.0)
+        for n in range(2):
+            nc.scalar.activation(windows[n][:], zeros[:, :1].bitcast(F32).to_broadcast([P, T]), SILU)
+
+        w1w, w2w, gates = {}, {}, {}
+
+        def load_scales(tile, rows):
+            for r in range(4):
+                nc.sync.dma_start(tile[r:P:32].bitcast(I32), rows[r:16:4].bitcast(I32))
 
         def load_w1_scales(e0, e1):
             load_scales(w1s[e0], w1_planes[:, e0 * PASSES:e1 * PASSES, :])
 
-        ident = keep.tile([P, P], F32, name="ident")
-        make_identity(nc, ident[:])
-        offsets = keep.tile([P, S // 16], U16, name="offsets")
-        nc.sync.dma_start(offsets[:], offs)
-        load_x(keep, 0, 1)
-        load_w1(keep, E, E + 1)
-        nc.vector.memset(xs[:].rearrange("p a w -> p (a w)").bitcast(I32), 0)
-        load_scales(xs, x_scales.rearrange("s f t -> f s t"))
-        zeros = keep.tile([P, ZW], I32, name="zeros", align_bytes=64)
-        nc.vector.memset(zeros[:], 0)
-        fill(w1s[E])
-        load_w1_scales(E, E + 1)
-        fill(w1s[4])
-        fill(w2s)
-        fill(w1s[0])
+        def load_w1(e):
+            w1w[e] = sbuf("w1w%d" % e, [P, PASSES, 2 * H], U8)
+            nc.sync.dma_start(w1w[e][:].bitcast(I32), w1_rows[:, e * PASSES:(e + 1) * PASSES, :])
 
-        late = stage(0)
-        for n in range(NT):
-            clear_window(n, 0)
-        load_x(late, 1, PASSES)
-        load_w1(late, 4, E)
+        def load_w2(e0, e1):
+            t = sbuf("w2w%d" % e0, [P, e1 - e0, 2 * N], U8)
+            nc.sync.dma_start(t[:].rearrange("p e b -> p (e b)").bitcast(I32).rearrange("p (e w) -> p e w", e=e1 - e0), w2_rows[:, e0:e1, :])
+            for e in range(e0, e1):
+                w2w[e] = t[:, e - e0, :]
+
+        def load_gate(e0, e1):
+            g = sbuf("gate%d" % e0, [P, (e1 - e0) * C], F32)
+            nc.sync.dma_start(g[:], gate[:P, e0 * C:e1 * C])
+            for e in range(e0, e1):
+                gates[e] = g[:, (e - e0) * C:(e - e0 + 1) * C]
+
+        nc.sync.dma_start(offsets[:], offs)
+        nc.sync.dma_start(xw[:, 0, :], x_rows[:, 0, :])
+        load_w1_scales(E, E + 1)
+        load_w1(E)
+        nc.sync.dma_start(xw[:, 1:, :LEAD], x_rows[:, 1:, :LEAD])
+        load_scales(xs, x_scales.rearrange("s f t -> f s t"))
+        nc.sync.dma_start(xw[:, 1:, LEAD:], x_rows[:, 1:, LEAD:])
+        load_w1_scales(0, E)
         load_scales(w2s, w2_scales.rearrange("e s f n -> f (e s) n"))
-        load_w1_scales(4, E)
-        load_w2(late, 4, E + 1)
-        load_gate(late, 0, E)
-        load_w1(late, 2, 4)
-        load_w1_scales(0, 4)
-        load_w1(late, 1, 2)
-        load_w1(late, 0, 1)
-        load_w2(late, 0, 4)
+        for e in (5, 4, 3):
+            load_w1(e)
+        load_w2(3, 6)
+        load_gate(3, 6)
+        load_w1(2)
+        load_w1(1)
+        load_w2(0, 3)
+        load_gate(0, 3)
+        load_w1(0)
+        load_w2(E, E + 1)
 
         gw, gs = {}, {}
 
-        def gather_words(e0, e1, s, tag=None):
-            name = "gw%d_%d" % (e0, s)
-            t = late.tile([P, (e1 - e0) * C], U32, name=name, tag=tag or name, align_bytes=64)
-            nc.vector.tensor_copy(t[:], xw[s].bitcast(U32).indirect(slots(e0, e1)))
+        def gather_words(e0, e1, s):
+            t = sbuf("gw%d_%d" % (e0, s), [P, (e1 - e0) * C], U32)
+            nc.vector.tensor_copy(t[:], xw[:, s, :].bitcast(U32).indirect(slots(e0, e1)))
             for e in range(e0, e1):
                 gw[e, s] = t[:, (e - e0) * C:(e - e0 + 1) * C]
 
-        def gather_scales(e0, e1, s0, s1, tag=None):
-            name = "gs%d_%d" % (e0, s0)
-            t = late.tile([P, s1 - s0, (e1 - e0) * C], U8, name=name, tag=tag or name, align_bytes=64)
-            for s in range(s0, s1):
-                nc.vector.tensor_copy(t[:, s - s0, :], xs[:, s, :].indirect(slots(e0, e1)))
-                for e in range(e0, e1):
-                    gs[e, s] = t[:, s - s0, (e - e0) * C:(e - e0 + 1) * C]
-            return t
+        gather_words(0, E, 0)
+        dealt_w = sbuf("dealt_w", [P, PASSES, H], U16)
+        dealt_s = sbuf("dealt_s", [P, PASSES, H], U8)
+        for s in range(PASSES):
+            nc.scalar.copy(dealt_w[:, s, :].rearrange("p (t m) -> p t m", t=4),
+                           w1w[E][:, s, :].bitcast(U16).rearrange("p (m t) -> p t m", t=4))
+        nc.gpsimd.tensor_copy(dealt_s[:].rearrange("p s (t m) -> p s t m", t=4),
+                              w1s[E][:].rearrange("p s (m t) -> p s t m", t=4))
+        for s in range(PASSES):
+            t = sbuf("gs%d" % s, [P, S], U8)
+            nc.vector.tensor_copy(t[:], xs[:, s, :].indirect(slots(0, E)))
+            for e in range(E):
+                gs[e, s] = t[:, e * C:(e + 1) * C]
+        for e0, e1 in ((4, E), (0, 4)):
+            for s in range(1, PASSES):
+                gather_words(e0, e1, s)
 
-        hb, codes = {}, {}
+        hb, grouped, codes, ys, gated = {}, {}, {}, {}, {}
 
-        def first_pass(a, i, s):
-            e = min(i, E)
-            if i < E:
-                words, scales = gw[i, s], gs[i, s]
-            else:
-                t0 = (i - E) * P
-                words, scales = xw[s][:, t0:t0 + P], xs[:, s, t0:t0 + P]
-            e0 = max(first for first, last in sets if first <= e)
-            w_scales = w1s[e0][:, (e - e0) * PASSES + s, :]
-            nc.tensor.matmul_mx(
-                out=a[:], lhsT=words.bitcast(FP8X4), lhsT_scale=scales,
-                rhs=w1w[e][:, s, :].bitcast(FP4X4), rhs_scale=w_scales,
-                start=(s == 0), stop=(s == PASSES - 1))
+        def layer1(e, b):
+            a = bank(b)
+            for s in range(PASSES):
+                nc.tensor.matmul_mx(
+                    out=a[:], lhsT=gw[e, s].bitcast(FP8X4), lhsT_scale=gs[e, s],
+                    rhs=w1w[e][:, s, :].bitcast(FP4X4), rhs_scale=w1s[0][:, e * PASSES + s, :],
+                    start=(s == 0), stop=(s == PASSES - 1))
+            hb[e] = sbuf("h%d" % e, [P, 2, P, 2], BF16)
+            nc.scalar.activation(hb[e][:], a[:].rearrange("t (p u e) -> t u p e", u=2, e=2), SILU)
 
-        def activate(a, i):
-            h = keep.tile([P, 2, P, 2], BF16, name="h%d" % i)
-            nc.scalar.activation(h[:], a[:].rearrange("t (p u e) -> t u p e", u=2, e=2), SILU)
-            hb[i] = h
+        def shared_tile(j, b, tiles=1, t0=0, t1=4):
+            a = bank(b)[:].rearrange("p (t c) -> p t c", t=t1 - t0)
+            tokens = slice(j * P, (j + tiles) * P)
+            for t in range(t0, t1):
+                cols = slice(t * P, (t + 1) * P)
+                for s in range(PASSES):
+                    nc.tensor.matmul_mx(
+                        out=a[:, t - t0, :], lhsT=dealt_w[:, s, cols].bitcast(U8).bitcast(FP4X4), lhsT_scale=dealt_s[:, s, cols],
+                        rhs=xw[:, s, tokens].bitcast(FP8X4), rhs_scale=xs[:, s, tokens],
+                        start=(s == 0), stop=(s == PASSES - 1))
+            dst = shared[j // 4][:, (j % 4) * H:(j % 4 + tiles) * H]
+            nc.scalar.activation(dst.rearrange("p (c t) -> p c t", t=4)[:, :, t0:t1], a.rearrange("p t c -> p c t"), SILU)
 
-        def layer1(i, b, opened=None):
-            a = bank(b) if opened is None else opened
-            for s in range(0 if opened is None else 1, PASSES):
-                first_pass(a, i, s)
-            activate(a, i)
-
-        def grouped(i0, i1):
-            return late.tile([P, (i1 - i0) * H], BF16, name="grouped%d" % i0, tag="grouped%d" % i0, align_bytes=64)
-
-        def turn(i0, i1, b, dst, copy):
+        def turn(i0, i1, b, dst, copy=nc.scalar.copy):
             tr = bank(b)[:].rearrange("p (h w t) -> p h w t", h=2, w=2)[:, :i1 - i0]
             for i in range(i0, i1):
                 words = hb[i][:].rearrange("t u p e -> t (u p e)").bitcast(F32)
@@ -192,116 +176,96 @@ def tile_moe_shr_mlp_silu_kernel(tc, x_words, x_scales, w1_words, w1_scales, w2_
                     nc.tensor.transpose(tr[:, i - i0, w, :], words[:, w * P:(w + 1) * P], ident[:])
             copy(dst.bitcast(F32).rearrange("p (h t w) -> p h t w", h=i1 - i0, w=2), tr.rearrange("p h w t -> p h t w"))
 
-        def quantise(i0, i1, src, tag=None):
-            hw = late.tile([P, (i1 - i0) * P], U32, name="hw%d" % i0, tag=tag or "hw%d" % i0, align_bytes=64)
-            hs = late.tile([P, (i1 - i0) * P], U8, name="hs%d" % i0, align_bytes=64)
-            nc.vector.quantize_mx(out=hw[:].bitcast(FP8X4), scales=hs[:], in_=src)
-            for i in range(i0, i1):
-                codes[i] = (hw, hs, i0)
+        def quantise(i0, i1, src):
+            hw = sbuf("hw%d" % i0, [P, (i1 - i0) * P], U32)[:]
+            hs = sbuf("hs%d" % i0, [P, (i1 - i0) * P], U8)
+            nc.vector.quantize_mx(out=hw.bitcast(FP8X4), scales=hs[:], in_=src)
+            codes[i0] = (hw, hs)
 
-        def turn_routed(e0, e1, b, copy):
-            g = grouped(e0, e1)
-            turn(e0, e1, b, g[:], copy)
-            quantise(e0, e1, g[:])
+        def turn_routed(e, b, copy=nc.scalar.copy):
+            grouped[e] = sbuf("grouped%d" % e, [P, H], BF16)
+            turn(e, e + 1, b, grouped[e][:], copy)
+            quantise(e, e + 1, grouped[e][:])
 
-        def layer2(dst, e, n, i0, i1):
-            hw, hs, first = codes[i0]
-            cols = slice((i0 - first) * P, (i1 - first) * P)
+        shared = [sbuf("grouped%d" % (E + 4 * half), [P, 4 * H], BF16) for half in range(2)]
+
+        def layer2(dst, e, n, i0):
+            hw, hs = codes[i0]
             nc.tensor.matmul_mx(
                 out=dst, lhsT=w2w[e][:, n * 2 * P:(n + 1) * 2 * P].bitcast(FP4X4),
                 lhsT_scale=w2s[:, e, n * P:(n + 1) * P],
-                rhs=hw[:, cols].bitcast(FP8X4), rhs_scale=hs[:, cols], start=True, stop=True)
+                rhs=hw.bitcast(FP8X4), rhs_scale=hs[:], start=True, stop=True)
 
-        ys = {}
+        def weigh(e, n0, n1, dst):
+            view = dst.rearrange("p (n c) -> p n c", c=C)
+            nc.vector.tensor_tensor(view, ys[e][:, n0:n1, :], gates[e].unsqueeze(1).to_broadcast([P, n1 - n0, C]), MULT)
+            for n in range(n0, n1):
+                gated[e, n] = view[:, n - n0, :]
 
-        gated = late.tile([P, NT, S], F32, name="gated", align_bytes=64)
+        def scatter(e, n, on_scalar):
+            dst = windows[n][:].indirect(slots(e, e + 1))
+            if on_scalar:
+                nc.scalar.activation(dst, gated[e, n], COPY)
+            else:
+                nc.vector.tensor_copy(dst, gated[e, n])
 
-        def second(e0, e1, n0, n1, b, step=1):
-            blocks = range(n0, n1, step)
-            y = bank(b)[:, :len(blocks) * (e1 - e0) * C].rearrange("p (n c) -> p n c", n=len(blocks))
-            for k, n in enumerate(blocks):
-                for e in range(e0, e1):
-                    layer2(y[:, k, (e - e0) * C:(e - e0 + 1) * C], e, n, e, e + 1)
-            g, first = gates[e0]
-            weights = g[:, (e0 - first) * C:(e1 - first) * C].unsqueeze(1).to_broadcast([P, len(blocks), (e1 - e0) * C])
-            nc.vector.tensor_tensor(gated[:, n0:n1:step, e0 * C:e1 * C], y, weights, MULT)
+        def second(e, b):
+            ys[e] = bank(b)[:, :N].rearrange("p (n c) -> p n c", n=NT)
+            for n in range(NT):
+                layer2(ys[e][:, n, :], e, n, e)
+            weigh(e, 0, NT, sbuf("gated%d" % e, [P, N], F32)[:])
 
-        def scatter(e0, e1, n, copy):
-            copy(windows[n][:].indirect(slots(e0, e1)), gated[:, n, e0 * C:e1 * C])
-
-        def by_scalar(dst, src):
-            nc.scalar.activation(dst, src, COPY)
+        def scatters(e, scalar_blocks):
+            for n in (0, 2, 1):
+                scatter(e, n, n in scalar_blocks)
 
         def finish(n, half, b, cuts):
             y = bank(b)
             t0 = half * BANK
-            layer2(y[:], E, n, E + 4 * half, E + 4 * half + 4)
+            layer2(y[:], E, n, E + 4 * half)
             for c0, c1 in zip(cuts, cuts[1:]):
-                res = keep.tile([P, c1 - c0], F32, name="res%d_%d" % (n, t0 + c0))
+                res = sbuf("res%d_%d" % (n, t0 + c0), [P, c1 - c0], F32)
                 nc.vector.tensor_tensor(res[:], y[:, c0:c1], windows[n][:, t0 + c0:t0 + c1], ADD)
                 nc.sync.dma_start(out[n * P:(n + 1) * P, t0 + c0:t0 + c1], res[:])
 
-        shared = [grouped(E, E + 4), grouped(E + 4, E + 8)]
+        for j in range(0, 6, 2):
+            shared_tile(j, j, 2, 0, 2)
+            shared_tile(j, j + 1, 2, 2, 4)
+            if j == 2:
+                quantise(E, E + 4, shared[0][:])
+        shared_tile(6, 6)
 
-        def turn_shared(pair, b, copy, tag=None):
-            i = E + 2 * pair
-            turn(i, i + 2, b, shared[pair // 2][:, (pair % 2) * 2 * H:(pair % 2 + 1) * 2 * H], copy)
-            if pair % 2 == 1:
-                quantise(i - 2, i + 2, shared[pair // 2][:], tag)
-
-        on_scalar, on_vector = nc.scalar.copy, nc.vector.tensor_copy
-
-        gather_words(0, E, 0)
-        gather_scales(2, E, 0, PASSES)
-        for s in range(1, PASSES):
-            gather_words(4, E, s)
-        for s in range(1, PASSES):
-            gather_words(0, 4, s)
-
-        opened = [bank(b) for b in range(4)]
-        for b in range(4):
-            first_pass(opened[b], E + b, 0)
-        for b in range(4):
-            layer1(E + b, b, opened[b])
-        layer1(E + 4, 0)
-        layer1(E + 5, 1)
-        layer1(5, 4)
-        layer1(4, 5)
-        gather_scales(0, 2, 0, PASSES, "gw4_2")
-        turn(E, E + 2, 4, shared[0][:, :2 * H], on_scalar)
-        turn_routed(4, E, 5, on_scalar)
-        layer1(E + 6, 4)
-        turn(E + 2, E + 4, 5, shared[0][:, 2 * H:], on_scalar)
-        second(4, E, 0, 1, 2)
-        scatter(4, E, 0, by_scalar)
-        second(4, E, 1, NT, 3)
-        scatter(4, E, 1, on_vector)
-        scatter(4, E, 2, on_vector)
-        quantise(E, E + 4, shared[0][:])
-        layer1(E + 7, 4)
-        layer1(3, 0)
-        layer1(2, 6)
-        layer1(1, 1)
-        turn_routed(2, 4, 7, on_vector)
-        layer1(0, 5)
-        turn(E + 4, E + 6, 0, shared[1][:, :2 * H], on_scalar)
-        turn(E + 6, E + 8, 6, shared[1][:, 2 * H:], on_scalar)
-        second(2, 4, 0, NT, 3, 2)
-        turn_routed(0, 2, 1, on_scalar)
-        scatter(2, 4, 0, by_scalar)
-        second(2, 4, 1, 2, 0)
-        scatter(2, 4, 1, by_scalar)
-        scatter(2, 4, 2, on_vector)
-        second(0, 2, 0, 2, 2)
-        scatter(0, 2, 0, by_scalar)
-        scatter(0, 2, 1, by_scalar)
-        second(0, 2, 2, 3, 7)
+        layer1(5, 7)
+        layer1(4, 0)
+        turn_routed(5, 1)
+        layer1(3, 2)
+        turn_routed(4, 3)
+        second(5, 4)
+        layer1(2, 5)
+        scatters(5, (0, 1))
+        turn_routed(3, 6, nc.vector.tensor_copy)
+        second(4, 1)
+        shared_tile(7, 7)
         quantise(E + 4, E + 8, shared[1][:])
-        scatter(0, 2, 2, on_vector)
+        layer1(1, 0)
+        scatters(4, (0, 1))
+        turn_routed(2, 3, nc.vector.tensor_copy)
+        second(3, 2)
+        layer1(0, 4)
+        scatters(3, (0, 1))
+        turn_routed(1, 5, nc.vector.tensor_copy)
+        second(2, 6)
+        turn_routed(0, 1, nc.vector.tensor_copy)
+        scatters(2, (0, 1))
+        second(1, 3)
+        second(0, 2)
+        scatters(1, (0, 1))
+        scatters(0, (0, 1))
+
         whole = (0, BANK)
-        finish(2, 0, 1, whole)
-        finish(2, 1, 5, whole)
-        finish(0, 0, 7, whole)
-        finish(0, 1, 2, whole)
-        finish(1, 0, 1, whole)
-        finish(1, 1, 5, (0, BANK - TAIL, BANK))
+        finish(2, 0, 7, whole)
+        finish(2, 1, 0, whole)
+        finish(0, 0, 4, whole)
+        finish(0, 1, 5, whole)
+        finish(1, 0, 6, whole)
+        finish(1, 1, 1, (0, BANK - TAIL, BANK))

@@ -109,13 +109,14 @@ def tile_moe_shr_mlp_silu_kernel(tc, x_words, x_scales, w1_words, w1_scales, w2_
         load_scales(w2s, w2_scales.rearrange("e s f n -> f (e s) n"))
         for e in (5, 4, 3):
             load_w1(e)
-        load_w2(3, 6)
+        load_w2(5, 6)
         load_gate(3, 6)
         load_w1(2)
+        load_w2(3, 5)
         load_w1(1)
+        load_w1(0)
         load_w2(0, 3)
         load_gate(0, 3)
-        load_w1(0)
         load_w2(E, E + 1)
 
         gw, gs = {}, {}

from contextlib import ExitStack

import concourse.mybir as mybir
from concourse.masks import make_identity

K, T, E, C, H, N = 1536, 1024, 6, 128, 512, 384
FLOPS = 2 * (T + E * C) * (K * H + H * N)

F32 = mybir.dt.float32
BF16 = mybir.dt.bfloat16
I32 = mybir.dt.int32
U32 = mybir.dt.uint32
U16 = mybir.dt.uint16
U8 = mybir.dt.uint8
FP8X4 = mybir.dt.float8_e4m3fn_x4
FP4X4 = mybir.dt.float4_e2m1fn_x4
SILU = mybir.ActivationFunctionType.Silu
COPY = mybir.ActivationFunctionType.Copy
MULT = mybir.AluOpType.mult
ADD = mybir.AluOpType.add

P = 128
PASSES = K // 512
NT = N // P
S = E * C
BANK = 512
LEAD = 256
TAIL = 128
ZW = 16


def tile_moe_shr_mlp_silu_kernel(tc, x_words, x_scales, w1_words, w1_scales, w2_words, w2_scales, gate, offs, out):
    nc = tc.nc
    with ExitStack() as ctx:
        keep = ctx.enter_context(tc.tile_pool(name="keep", bufs=1))
        psum = ctx.enter_context(tc.psum_pool(name="psum", bufs=1))

        banks = [psum.tile([P, BANK], F32, name="bank%d" % b) for b in range(8)]

        def bank(b):
            return banks[b]

        def sbuf(name, shape, dtype):
            return keep.tile(shape, dtype, name=name, align_bytes=64)

        def slots(e0, e1):
            return offsets[:, e0 * C // 16:e1 * C // 16]

        x_rows = x_words.rearrange("s p t r -> p s (t r)").bitcast(I32)
        w1_rows = w1_words.rearrange("e s p b -> p (e s) b").bitcast(I32)
        w2_rows = w2_words.rearrange("e s p b -> p (e s) b").bitcast(I32)
        w1_planes = w1_scales.rearrange("e s f i -> f (e s) i")

        offsets = keep.tile([P, S // 16], U16, name="offsets")
        xw = sbuf("xw", [P, PASSES, T], I32)
        xs = sbuf("xs", [P, PASSES, T], U8)
        w2s = sbuf("w2s", [P, E + 1, N], U8)
        sets = ((E, E + 1), (0, E))
        w1s = {e0: sbuf("w1s%d" % e0, [P, (e1 - e0) * PASSES, H], U8) for e0, e1 in sets}
        zeros = sbuf("zeros", [P, ZW], I32)
        ident = sbuf("ident", [P, P], F32)
        windows = [sbuf("win%d" % n, [P, T], F32) for n in range(NT)]

        nc.gpsimd.memset(w1s[E][:].rearrange("p a w -> p (a w)").bitcast(I32), 0)
        nc.vector.memset(xs[:].rearrange("p a w -> p (a w)").bitcast(I32), 0)
        nc.vector.memset(zeros[:], 0)
        for tile in (w1s[0], w2s):
            words = tile[:].rearrange("p a w -> p (a w)").bitcast(I32)
            nc.vector.tensor_copy(words.rearrange("p (c w) -> p c w", w=ZW),
                                  zeros[:].unsqueeze(1).to_broadcast([P, words.shape[1] // ZW, ZW]))
        make_identity(nc, ident[:])
        nc.gpsimd.memset(windows[2][:], 0.0)
        for n in range(2):
            nc.scalar.activation(windows[n][:], zeros[:, :1].bitcast(F32).to_broadcast([P, T]), SILU)

        w1w, w2w, gates = {}, {}, {}

        def load_scales(tile, rows):
            for r in range(4):
                nc.sync.dma_start(tile[r:P:32].bitcast(I32), rows[r:16:4].bitcast(I32))

        def load_w1_scales(e0, e1):
            load_scales(w1s[e0], w1_planes[:, e0 * PASSES:e1 * PASSES, :])

        def load_w1(e):
            w1w[e] = sbuf("w1w%d" % e, [P, PASSES, 2 * H], U8)
            nc.sync.dma_start(w1w[e][:].bitcast(I32), w1_rows[:, e * PASSES:(e + 1) * PASSES, :])

        def load_w2(e0, e1):
            t = sbuf("w2w%d" % e0, [P, e1 - e0, 2 * N], U8)
            nc.sync.dma_start(t[:].rearrange("p e b -> p (e b)").bitcast(I32).rearrange("p (e w) -> p e w", e=e1 - e0), w2_rows[:, e0:e1, :])
            for e in range(e0, e1):
                w2w[e] = t[:, e - e0, :]

        def load_gate(e0, e1):
            g = sbuf("gate%d" % e0, [P, (e1 - e0) * C], F32)
            nc.sync.dma_start(g[:], gate[:P, e0 * C:e1 * C])
            for e in range(e0, e1):
                gates[e] = g[:, (e - e0) * C:(e - e0 + 1) * C]

        nc.sync.dma_start(offsets[:], offs)
        nc.sync.dma_start(xw[:, 0, :], x_rows[:, 0, :])
        load_w1_scales(E, E + 1)
        load_w1(E)
        nc.sync.dma_start(xw[:, 1:, :LEAD], x_rows[:, 1:, :LEAD])
        load_scales(xs, x_scales.rearrange("s f t -> f s t"))
        nc.sync.dma_start(xw[:, 1:, LEAD:], x_rows[:, 1:, LEAD:])
        load_w1_scales(0, E)
        load_scales(w2s, w2_scales.rearrange("e s f n -> f (e s) n"))
        for e in (5, 4, 3):
            load_w1(e)
        load_w2(5, 6)
        load_gate(3, 6)
        load_w1(2)
        load_w2(3, 5)
        load_w1(1)
        load_w1(0)
        load_w2(0, 3)
        load_gate(0, 3)
        load_w2(E, E + 1)

        gw, gs = {}, {}

        def gather_words(e0, e1, s):
            t = sbuf("gw%d_%d" % (e0, s), [P, (e1 - e0) * C], U32)
            nc.vector.tensor_copy(t[:], xw[:, s, :].bitcast(U32).indirect(slots(e0, e1)))
            for e in range(e0, e1):
                gw[e, s] = t[:, (e - e0) * C:(e - e0 + 1) * C]

        gather_words(0, E, 0)
        dealt_w = sbuf("dealt_w", [P, PASSES, H], U16)
        dealt_s = sbuf("dealt_s", [P, PASSES, H], U8)
        for s in range(PASSES):
            nc.scalar.copy(dealt_w[:, s, :].rearrange("p (t m) -> p t m", t=4),
                           w1w[E][:, s, :].bitcast(U16).rearrange("p (m t) -> p t m", t=4))
        nc.gpsimd.tensor_copy(dealt_s[:].rearrange("p s (t m) -> p s t m", t=4),
                              w1s[E][:].rearrange("p s (m t) -> p s t m", t=4))
        for s in range(PASSES):
            t = sbuf("gs%d" % s, [P, S], U8)
            nc.vector.tensor_copy(t[:], xs[:, s, :].indirect(slots(0, E)))
            for e in range(E):
                gs[e, s] = t[:, e * C:(e + 1) * C]
        for e0, e1 in ((4, E), (0, 4)):
            for s in range(1, PASSES):
                gather_words(e0, e1, s)

        hb, grouped, codes, ys, gated = {}, {}, {}, {}, {}

        def layer1(e, b):
            a = bank(b)
            for s in range(PASSES):
                nc.tensor.matmul_mx(
                    out=a[:], lhsT=gw[e, s].bitcast(FP8X4), lhsT_scale=gs[e, s],
                    rhs=w1w[e][:, s, :].bitcast(FP4X4), rhs_scale=w1s[0][:, e * PASSES + s, :],
                    start=(s == 0), stop=(s == PASSES - 1))
            hb[e] = sbuf("h%d" % e, [P, 2, P, 2], BF16)
            nc.scalar.activation(hb[e][:], a[:].rearrange("t (p u e) -> t u p e", u=2, e=2), SILU)

        def shared_tile(j, b, tiles=1, t0=0, t1=4):
            a = bank(b)[:].rearrange("p (t c) -> p t c", t=t1 - t0)
            tokens = slice(j * P, (j + tiles) * P)
            for t in range(t0, t1):
                cols = slice(t * P, (t + 1) * P)
                for s in range(PASSES):
                    nc.tensor.matmul_mx(
                        out=a[:, t - t0, :], lhsT=dealt_w[:, s, cols].bitcast(U8).bitcast(FP4X4), lhsT_scale=dealt_s[:, s, cols],
                        rhs=xw[:, s, tokens].bitcast(FP8X4), rhs_scale=xs[:, s, tokens],
                        start=(s == 0), stop=(s == PASSES - 1))
            dst = shared[j // 4][:, (j % 4) * H:(j % 4 + tiles) * H]
            nc.scalar.activation(dst.rearrange("p (c t) -> p c t", t=4)[:, :, t0:t1], a.rearrange("p t c -> p c t"), SILU)

        def turn(i0, i1, b, dst, copy=nc.scalar.copy):
            tr = bank(b)[:].rearrange("p (h w t) -> p h w t", h=2, w=2)[:, :i1 - i0]
            for i in range(i0, i1):
                words = hb[i][:].rearrange("t u p e -> t (u p e)").bitcast(F32)
                for w in range(2):
                    nc.tensor.transpose(tr[:, i - i0, w, :], words[:, w * P:(w + 1) * P], ident[:])
            copy(dst.bitcast(F32).rearrange("p (h t w) -> p h t w", h=i1 - i0, w=2), tr.rearrange("p h w t -> p h t w"))

        def quantise(i0, i1, src):
            hw = sbuf("hw%d" % i0, [P, (i1 - i0) * P], U32)[:]
            hs = sbuf("hs%d" % i0, [P, (i1 - i0) * P], U8)
            nc.vector.quantize_mx(out=hw.bitcast(FP8X4), scales=hs[:], in_=src)
            codes[i0] = (hw, hs)

        def turn_routed(e, b, copy=nc.scalar.copy):
            grouped[e] = sbuf("grouped%d" % e, [P, H], BF16)
            turn(e, e + 1, b, grouped[e][:], copy)
            quantise(e, e + 1, grouped[e][:])

        shared = [sbuf("grouped%d" % (E + 4 * half), [P, 4 * H], BF16) for half in range(2)]

        def layer2(dst, e, n, i0):
            hw, hs = codes[i0]
            nc.tensor.matmul_mx(
                out=dst, lhsT=w2w[e][:, n * 2 * P:(n + 1) * 2 * P].bitcast(FP4X4),
                lhsT_scale=w2s[:, e, n * P:(n + 1) * P],
                rhs=hw.bitcast(FP8X4), rhs_scale=hs[:], start=True, stop=True)

        def weigh(e, n0, n1, dst):
            view = dst.rearrange("p (n c) -> p n c", c=C)
            nc.vector.tensor_tensor(view, ys[e][:, n0:n1, :], gates[e].unsqueeze(1).to_broadcast([P, n1 - n0, C]), MULT)
            for n in range(n0, n1):
                gated[e, n] = view[:, n - n0, :]

        def scatter(e, n, on_scalar):
            dst = windows[n][:].indirect(slots(e, e + 1))
            if on_scalar:
                nc.scalar.activation(dst, gated[e, n], COPY)
            else:
                nc.vector.tensor_copy(dst, gated[e, n])

        def second(e, b):
            ys[e] = bank(b)[:, :N].rearrange("p (n c) -> p n c", n=NT)
            for n in range(NT):
                layer2(ys[e][:, n, :], e, n, e)
            weigh(e, 0, NT, sbuf("gated%d" % e, [P, N], F32)[:])

        def scatters(e, scalar_blocks):
            for n in (0, 2, 1):
                scatter(e, n, n in scalar_blocks)

        def finish(n, half, b, cuts):
            y = bank(b)
            t0 = half * BANK
            layer2(y[:], E, n, E + 4 * half)
            for c0, c1 in zip(cuts, cuts[1:]):
                res = sbuf("res%d_%d" % (n, t0 + c0), [P, c1 - c0], F32)
                nc.vector.tensor_tensor(res[:], y[:, c0:c1], windows[n][:, t0 + c0:t0 + c1], ADD)
                nc.sync.dma_start(out[n * P:(n + 1) * P, t0 + c0:t0 + c1], res[:])

        for j in range(0, 6, 2):
            shared_tile(j, j, 2, 0, 2)
            shared_tile(j, j + 1, 2, 2, 4)
            if j == 2:
                quantise(E, E + 4, shared[0][:])
        shared_tile(6, 6)

        layer1(5, 7)
        layer1(4, 0)
        turn_routed(5, 1)
        layer1(3, 2)
        turn_routed(4, 3)
        second(5, 4)
        layer1(2, 5)
        scatters(5, (0, 1))
        turn_routed(3, 6, nc.vector.tensor_copy)
        second(4, 1)
        shared_tile(7, 7)
        quantise(E + 4, E + 8, shared[1][:])
        layer1(1, 0)
        scatters(4, (0, 1))
        turn_routed(2, 3, nc.vector.tensor_copy)
        second(3, 2)
        layer1(0, 4)
        scatters(3, (0, 1))
        turn_routed(1, 5, nc.vector.tensor_copy)
        second(2, 6)
        turn_routed(0, 1, nc.vector.tensor_copy)
        scatters(2, (0, 1))
        second(1, 3)
        second(0, 2)
        scatters(1, (0, 1))
        scatters(0, (0, 1))

        whole = (0, BANK)
        finish(2, 0, 7, whole)
        finish(2, 1, 0, whole)
        finish(0, 0, 4, whole)
        finish(0, 1, 5, whole)
        finish(1, 0, 6, whole)
        finish(1, 1, 1, (0, BANK - TAIL, BANK))
